import numpy as np
import ml_dtypes


def mxq(x, axis, fmt="e4m3"):
    dtype, down = {"e4m3": (ml_dtypes.float8_e4m3fn, 7), "e5m2": (ml_dtypes.float8_e5m2, 14)}[fmt]
    v = np.moveaxis(np.asarray(x, np.float32).astype(ml_dtypes.bfloat16).astype(np.float64), axis, -1)
    blocks = v.reshape(v.shape[:-1] + (-1, 32))
    amax = np.abs(blocks).max(-1, keepdims=True)
    byte = np.maximum(np.where(amax > 0, np.frexp(amax)[1] - 1 + 127, 0) - down, 1)
    scale = np.exp2(byte - 127.0)
    codes = (blocks / scale).astype(np.float32).astype(dtype).astype(np.float64)
    return np.moveaxis((codes * scale).reshape(v.shape), -1, axis)


WIDE = False


def mx_kscale(k):
    if not WIDE:
        return np.ones(k)
    levels = np.array([10, -10, 5, -5, 0])
    if k % 512:
        return np.exp2(np.random.permutation(np.resize(levels, k // 32))).repeat(32)
    a = np.empty((k // 512, 16))
    for p in range(k // 512):
        a[p, :8] = np.random.permutation(np.resize(levels, 8))
        for g in range(8):
            far = levels[np.abs(levels - a[p, g]) >= 10]
            a[p, g + 8] = far[np.random.randint(len(far))]
    return np.exp2(a.ravel()).repeat(32)


def f64(x):
    return np.asarray(x).astype(np.float64)


def striped(idx):
    return np.tile(idx.reshape(-1, 16).T, (8, 1)).astype(np.uint16)


def unstriped(offs):
    return offs[:16].T.reshape(-1).astype(np.int64)


def pack_weight(w):
    k, n = w.shape
    w = f64(np.asarray(w, np.float32).astype(ml_dtypes.bfloat16)).reshape(k // 32, 32, n)
    amax = np.abs(w).max(1)
    byte = np.clip(np.where(amax > 0, np.frexp(amax)[1] - 1 + 127 - 7, 1), 1, 254)
    scaled = (w * np.exp2(127.0 - byte)[:, None, :]).reshape(k, n).astype(np.float32)
    words = np.ascontiguousarray(scaled.reshape(k // 512, 128, 4, n).transpose(0, 1, 3, 2)).astype(ml_dtypes.float8_e4m3fn).view(np.uint8)
    return words, np.ascontiguousarray(byte.astype(np.uint8).reshape(k // 512, 16, n))


def unpack_weight(words, scales):
    g, p, n, _ = words.shape
    vals = np.ascontiguousarray(words).view(ml_dtypes.float8_e4m3fn).astype(np.float64) * np.repeat(np.exp2(scales.astype(np.float64) - 127.0), 8, axis=1)[..., None]
    return vals.transpose(0, 1, 3, 2).reshape(g * 512, n)


def silu(v):
    return v / (1.0 + np.exp(-np.maximum(v, -700.0)))


K, T, S, H, N = 1024, 1024, 512, 512, 128
P = 2 ** 7


def setup_inputs():
    n = np.random.standard_normal
    s = mx_kscale(K)[:, None]
    u = mx_kscale(H)
    packed_xT = pack_weight(n((K, T)) * s)
    packed_w2 = pack_weight(n((H, N)) / np.sqrt(H) / u[:, None])
    return {
        "x_words": packed_xT[0],
        "x_scales": packed_xT[1],
        "gate": np.tile(np.random.uniform(0.2, 1.0, T), (P, 1)).astype(np.float32),
        "w1": (n((K, H)) / np.sqrt(K) / s * u).astype(np.float32),
        "w2_words": packed_w2[0],
        "w2_scales": packed_w2[1],
        "offs": striped(np.random.permutation(T)[:S]),
    }


def reference(x_words, x_scales, gate, w1, w2_words, w2_scales, offs):
    xq = unpack_weight(x_words, x_scales)[:, unstriped(offs)]
    h = silu(mxq(f64(w1), 0, "e4m3").T @ xq)
    y = unpack_weight(w2_words, w2_scales).T @ mxq(h, 0, "e4m3")
    g = f64(gate)[:1][:, unstriped(offs)]
    out = np.zeros((N, T))
    out[:, unstriped(offs)] = y * g
    return out

@@ -1,0 +1,174 @@
+from contextlib import ExitStack
+
+import concourse.mybir as mybir
+
+K, T, S, H, N = 1024, 1024, 512, 512, 128
+FLOPS = 2 * S * H * (K + N)
+
+F32 = mybir.dt.float32
+BF16 = mybir.dt.bfloat16
+I32 = mybir.dt.int32
+U32 = mybir.dt.uint32
+U16 = mybir.dt.uint16
+U8 = mybir.dt.uint8
+FP8X4 = mybir.dt.float8_e4m3fn_x4
+SILU = mybir.ActivationFunctionType.Silu
+MULT = mybir.AluOpType.mult
+
+P = 128
+PACK = 4
+PASSES = K // (P * PACK)
+HALVES = 2
+HALF_M = P // HALVES
+CHUNK = 128
+CHUNKS = S // CHUNK
+LIST_COLS = CHUNK // 16
+LAST_SCALAR_M = 24
+IDENTITY = mybir.ActivationFunctionType.Identity
+
+
+def tile_picked_modgate_mlpsilu_p_kernel(tc, x_words, x_scales, gate, w1, w2_words, w2_scales, offs, out):
+    nc = tc.nc
+    with ExitStack() as ctx:
+        keep = ctx.enter_context(tc.tile_pool(name="keep", bufs=1))
+        psum = ctx.enter_context(tc.psum_pool(name="psum", bufs=1))
+
+        x_table = [
+            keep.tile([P, T], I32, name=f"x_table{g}", tag=f"x_table{g}", align_bytes=64) for g in range(PASSES)
+        ]
+        w1_raw = [
+            [keep.tile([P, PACK, H // HALVES], F32, name=f"w1_raw{g}{c}", align_bytes=64) for c in range(HALVES)]
+            for g in range(PASSES)
+        ]
+
+        def load_x(g):
+            nc.sync.dma_start(x_table[g][:], x_words[g].rearrange("p n t -> p (n t)").bitcast(I32))
+
+        load_x(0)
+        offsets = keep.tile([P, S // 16], U16, name="offsets")
+        nc.sync.dma_start(offsets[:], offs)
+
+        x_planes = keep.tile([P, T], U8, name="x_planes", align_bytes=64)
+        nc.gpsimd.memset(x_planes[:].bitcast(I32), 0)
+        for q in range(4):
+            nc.scalar.dma_start(
+                x_planes[32 * q : 32 * q + 4 * PASSES, :].bitcast(I32),
+                x_scales[:, 4 * q : 4 * q + 4, :].bitcast(I32),
+            )
+        warm = keep.tile([P, 1], F32, name="warm")
+        warm_out = keep.tile([P, 1], F32, name="warm_out")
+        nc.vector.memset(warm[:], 0.0)
+        nc.scalar.activation(warm_out[:], warm[:], SILU)
+
+        for g in range(PASSES):
+            rows = w1[g * P * PACK : (g + 1) * P * PACK, :].rearrange("(p j) h -> p j h", j=PACK)
+            for c in range(HALVES):
+                nc.sync.dma_start(w1_raw[g][c][:], rows[:, :, c * (H // HALVES) : (c + 1) * (H // HALVES)])
+        load_x(1)
+        gate_table = keep.tile([P, T], F32, name="gate_table", align_bytes=64)
+        nc.sync.dma_start(gate_table[:], gate)
+        w2_codes = keep.tile([P, N], I32, name="w2_codes", align_bytes=64)
+        nc.sync.dma_start(w2_codes[:], w2_words[0].rearrange("p n t -> p (n t)").bitcast(I32))
+
+        w2_plane = keep.tile([P, N], U8, name="w2_plane", align_bytes=64)
+        nc.gpsimd.memset(w2_plane[:].bitcast(I32), 0)
+        for q in range(4):
+            nc.gpsimd.dma_start(
+                w2_plane[32 * q : 32 * q + 4, :].bitcast(I32),
+                w2_scales[0, 4 * q : 4 * q + 4, :].bitcast(I32),
+            )
+
+        zero_bias = [
+            keep.tile([P, 1], F32, name=f"zero_bias{u}", tag=f"h{u + 2}", align_bytes=64) for u in range(CHUNKS - 2)
+        ]
+        for zero in zero_bias:
+            nc.gpsimd.memset(zero[:], 0.0)
+        window = keep.tile([P, T], F32, name="window", align_bytes=64)
+        nc.vector.memset(window[:], 0.0)
+
+        picked_planes = keep.tile([P, S], U8, name="picked_planes", align_bytes=64)
+        nc.vector.tensor_copy(picked_planes[:], x_planes[:].indirect(offsets[:]))
+        picked0 = keep.tile([P, S], U32, name="picked0", align_bytes=64)
+        nc.vector.tensor_copy(picked0[:], x_table[0][:].bitcast(U32).indirect(offsets[:]))
+
+        w1_codes = [keep.tile([P, PACK, P], U32, name=f"w1_codes{g}", align_bytes=64) for g in range(PASSES)]
+        w1_planes = [keep.tile([P, PACK, P], U8, name=f"w1_planes{g}", align_bytes=64) for g in range(PASSES)]
+
+        def quantise_w1(g):
+            for c in range(HALVES):
+                dealt = keep.tile([P, PACK, HALF_M, PACK], BF16, name=f"dealt{g}{c}", tag=f"dealt{c}", align_bytes=64)
+                src = w1_raw[g][c][:].rearrange("p j (m t) -> p m j t", t=PACK)
+                dst = dealt[:].rearrange("p t m j -> p m j t")
+                if (g, c) == (PASSES - 1, HALVES - 1):
+                    nc.scalar.copy(dst[:, :LAST_SCALAR_M], src[:, :LAST_SCALAR_M])
+                    nc.vector.tensor_copy(dst[:, LAST_SCALAR_M:], src[:, LAST_SCALAR_M:])
+                else:
+                    nc.scalar.copy(dst, src)
+                cols = slice(c * HALF_M, (c + 1) * HALF_M)
+                for t in range(PACK):
+                    nc.vector.quantize_mx(
+                        out=w1_codes[g][:, t, cols].bitcast(FP8X4),
+                        scales=w1_planes[g][:, t, cols],
+                        in_=dealt[:, t].rearrange("p m j -> p (m j)"),
+                    )
+
+        h_banks = [psum.tile([P, PACK, CHUNK], F32, name=f"h_bank{u}") for u in range(CHUNKS)]
+
+        def first_product(u, g, words):
+            tokens = slice(u * CHUNK, (u + 1) * CHUNK)
+            for t in range(PACK):
+                nc.tensor.matmul_mx(
+                    out=h_banks[u][:, t, :],
+                    lhsT=w1_codes[g][:, t, :].bitcast(FP8X4),
+                    lhsT_scale=w1_planes[g][:, t, :],
+                    rhs=words[:, tokens].bitcast(FP8X4),
+                    rhs_scale=picked_planes[4 * g :, tokens],
+                    start=(g == 0 and t == 0),
+                    stop=(g == PASSES - 1 and t == PACK - 1),
+                )
+
+        quantise_w1(0)
+        for u in range(CHUNKS):
+            first_product(u, 0, picked0)
+        quantise_w1(1)
+
+        entries = [offsets[:, u * LIST_COLS : (u + 1) * LIST_COLS] for u in range(CHUNKS)]
+        picked1 = keep.tile([P, S], U32, name="picked1", tag="dealt1", align_bytes=64)
+        for u in range(CHUNKS):
+            nc.vector.tensor_copy(
+                picked1[:, u * CHUNK : (u + 1) * CHUNK], x_table[1][:].bitcast(U32).indirect(entries[u])
+            )
+        scores_first = keep.tile([P, CHUNK], F32, name="scores_first", tag="x_table1", align_bytes=64)
+        nc.vector.tensor_copy(scores_first[:], gate_table[:].indirect(entries[0]))
+
+        for u in range(CHUNKS):
+            first_product(u, 1, picked1)
+            h = keep.tile([P, CHUNK, PACK], BF16, name=f"h{u}", tag=f"h{u}", align_bytes=64)
+            nc.scalar.activation(h[:], h_banks[u][:].rearrange("p t n -> p n t"), SILU)
+            h_codes = keep.tile([P, CHUNK], U32, name=f"h_codes{u}", align_bytes=64)
+            h_plane = keep.tile([P, CHUNK], U8, name=f"h_plane{u}", align_bytes=64)
+            nc.vector.quantize_mx(
+                out=h_codes[:].bitcast(FP8X4), scales=h_plane[:], in_=h[:].rearrange("p n t -> p (n t)")
+            )
+            if u == 0:
+                scores_rest = keep.tile([P, S - CHUNK], F32, name="scores_rest", tag="h0", align_bytes=64)
+                nc.vector.tensor_copy(scores_rest[:], gate_table[:].indirect(offsets[:, LIST_COLS:]))
+            y_bank = psum.tile([P, CHUNK], F32, name=f"y_bank{u}")
+            nc.tensor.matmul_mx(
+                out=y_bank[:],
+                lhsT=w2_codes[:].bitcast(FP8X4),
+                lhsT_scale=w2_plane[:],
+                rhs=h_codes[:].bitcast(FP8X4),
+                rhs_scale=h_plane[:],
+                start=True,
+                stop=True,
+            )
+            y = keep.tile([P, CHUNK], F32, name=f"y{u}", align_bytes=64)
+            if u + 2 < CHUNKS:
+                nc.scalar.activation(y[:], y_bank[:], IDENTITY, bias=zero_bias[u][:])
+            else:
+                nc.scalar.copy(y[:], y_bank[:])
+            scores = scores_first[:] if u == 0 else scores_rest[:, (u - 1) * CHUNK : u * CHUNK]
+            nc.vector.tensor_tensor(window[:].indirect(entries[u]), y[:], scores, MULT)
+
+        nc.sync.dma_start(out, window[:])

@@ -1,6 +1,7 @@
 from contextlib import ExitStack
 
 import concourse.mybir as mybir
+from concourse.masks import make_identity
 
 K, T, S, H, N = 1024, 1024, 512, 512, 128
 FLOPS = 2 * S * H * (K + N)
@@ -13,18 +14,19 @@ U16 = mybir.dt.uint16
 U8 = mybir.dt.uint8
 FP8X4 = mybir.dt.float8_e4m3fn_x4
 SILU = mybir.ActivationFunctionType.Silu
+IDENTITY = mybir.ActivationFunctionType.Identity
 MULT = mybir.AluOpType.mult
 
 P = 128
 PACK = 4
 PASSES = K // (P * PACK)
-HALVES = 2
-HALF_M = P // HALVES
 CHUNK = 128
 CHUNKS = S // CHUNK
 LIST_COLS = CHUNK // 16
-LAST_SCALAR_M = 24
-IDENTITY = mybir.ActivationFunctionType.Identity
+SCALAR_M = [84, 72]
+EARLY = 2
+GATE_COLS = T // P
+PER_BANK = 4
 
 
 def tile_picked_modgate_mlpsilu_p_kernel(tc, x_words, x_scales, gate, w1, w2_words, w2_scales, offs, out):
@@ -32,21 +34,6 @@ def tile_picked_modgate_mlpsilu_p_kernel(tc, x_words, x_scales, gate, w1, w2_wor
     with ExitStack() as ctx:
         keep = ctx.enter_context(tc.tile_pool(name="keep", bufs=1))
         psum = ctx.enter_context(tc.psum_pool(name="psum", bufs=1))
-
-        x_table = [
-            keep.tile([P, T], I32, name=f"x_table{g}", tag=f"x_table{g}", align_bytes=64) for g in range(PASSES)
-        ]
-        w1_raw = [
-            [keep.tile([P, PACK, H // HALVES], F32, name=f"w1_raw{g}{c}", align_bytes=64) for c in range(HALVES)]
-            for g in range(PASSES)
-        ]
-
-        def load_x(g):
-            nc.sync.dma_start(x_table[g][:], x_words[g].rearrange("p n t -> p (n t)").bitcast(I32))
-
-        load_x(0)
-        offsets = keep.tile([P, S // 16], U16, name="offsets")
-        nc.sync.dma_start(offsets[:], offs)
 
         x_planes = keep.tile([P, T], U8, name="x_planes", align_bytes=64)
         nc.gpsimd.memset(x_planes[:].bitcast(I32), 0)
@@ -57,60 +44,77 @@ def tile_picked_modgate_mlpsilu_p_kernel(tc, x_words, x_scales, gate, w1, w2_wor
             )
         warm = keep.tile([P, 1], F32, name="warm")
         warm_out = keep.tile([P, 1], F32, name="warm_out")
-        nc.vector.memset(warm[:], 0.0)
+        nc.gpsimd.memset(warm[:], 0.0)
         nc.scalar.activation(warm_out[:], warm[:], SILU)
 
+        x_table = [keep.tile([P, T], I32, name=f"x_table{g}", align_bytes=64) for g in range(PASSES)]
+        w1_raw = [keep.tile([P, PACK, H], F32, name=f"w1_raw{g}", align_bytes=64) for g in range(PASSES)]
+
+        def load_x(g):
+            nc.sync.dma_start(x_table[g][:], x_words[g].rearrange("p n t -> p (n t)").bitcast(I32))
+
+        gate_row = keep.tile([P, GATE_COLS], F32, name="gate_row", tag="dealt0", align_bytes=64)
+        nc.sync.dma_start(gate_row[:], gate[0].rearrange("(p c) -> p c", c=GATE_COLS))
+        offsets = keep.tile([P, S // 16], U16, name="offsets")
+        nc.sync.dma_start(offsets[:], offs)
         for g in range(PASSES):
             rows = w1[g * P * PACK : (g + 1) * P * PACK, :].rearrange("(p j) h -> p j h", j=PACK)
-            for c in range(HALVES):
-                nc.sync.dma_start(w1_raw[g][c][:], rows[:, :, c * (H // HALVES) : (c + 1) * (H // HALVES)])
-        load_x(1)
-        gate_table = keep.tile([P, T], F32, name="gate_table", align_bytes=64)
-        nc.sync.dma_start(gate_table[:], gate)
+            nc.sync.dma_start(w1_raw[g][:], rows)
+        for g in range(PASSES):
+            load_x(g)
         w2_codes = keep.tile([P, N], I32, name="w2_codes", align_bytes=64)
         nc.sync.dma_start(w2_codes[:], w2_words[0].rearrange("p n t -> p (n t)").bitcast(I32))
 
-        w2_plane = keep.tile([P, N], U8, name="w2_plane", align_bytes=64)
-        nc.gpsimd.memset(w2_plane[:].bitcast(I32), 0)
-        for q in range(4):
-            nc.gpsimd.dma_start(
-                w2_plane[32 * q : 32 * q + 4, :].bitcast(I32),
-                w2_scales[0, 4 * q : 4 * q + 4, :].bitcast(I32),
-            )
-
+        identity = keep.tile([P, P], F32, name="identity", align_bytes=64)
+        make_identity(nc, identity[:])
         zero_bias = [
             keep.tile([P, 1], F32, name=f"zero_bias{u}", tag=f"h{u + 2}", align_bytes=64) for u in range(CHUNKS - 2)
         ]
         for zero in zero_bias:
             nc.gpsimd.memset(zero[:], 0.0)
+        w2_plane = keep.tile([P, N], U8, name="w2_plane", align_bytes=64)
+        nc.gpsimd.memset(w2_plane[:].bitcast(I32), 0)
+        for q in range(4):
+            nc.sync.dma_start(
+                w2_plane[32 * q : 32 * q + 4, :].bitcast(I32),
+                w2_scales[0, 4 * q : 4 * q + 4, :].bitcast(I32),
+            )
+
         window = keep.tile([P, T], F32, name="window", align_bytes=64)
         nc.vector.memset(window[:], 0.0)
 
+        gate_table = keep.tile([P, T], F32, name="gate_table", tag="dealt1", align_bytes=64)
+        gate_view = gate_table[:].rearrange("p (n c) -> p n c", c=GATE_COLS)
+        for b in range(GATE_COLS // PER_BANK):
+            spread = psum.tile([P, PER_BANK, P], F32, name=f"spread{b}", tag=f"y_bank{b}")
+            for c in range(PER_BANK):
+                col = b * PER_BANK + c
+                nc.tensor.transpose(spread[:, c, :], gate_row[:, col : col + 1].to_broadcast([P, P]), identity[:])
+            nc.scalar.copy(gate_view[:, :, b * PER_BANK : (b + 1) * PER_BANK], spread[:].rearrange("p c n -> p n c"))
+
         picked_planes = keep.tile([P, S], U8, name="picked_planes", align_bytes=64)
         nc.vector.tensor_copy(picked_planes[:], x_planes[:].indirect(offsets[:]))
-        picked0 = keep.tile([P, S], U32, name="picked0", align_bytes=64)
-        nc.vector.tensor_copy(picked0[:], x_table[0][:].bitcast(U32).indirect(offsets[:]))
+        scores = keep.tile([P, S], F32, name="scores", align_bytes=64)
+        nc.vector.tensor_copy(scores[:], gate_table[:].indirect(offsets[:]))
 
         w1_codes = [keep.tile([P, PACK, P], U32, name=f"w1_codes{g}", align_bytes=64) for g in range(PASSES)]
         w1_planes = [keep.tile([P, PACK, P], U8, name=f"w1_planes{g}", align_bytes=64) for g in range(PASSES)]
 
-        def quantise_w1(g):
-            for c in range(HALVES):
-                dealt = keep.tile([P, PACK, HALF_M, PACK], BF16, name=f"dealt{g}{c}", tag=f"dealt{c}", align_bytes=64)
-                src = w1_raw[g][c][:].rearrange("p j (m t) -> p m j t", t=PACK)
-                dst = dealt[:].rearrange("p t m j -> p m j t")
-                if (g, c) == (PASSES - 1, HALVES - 1):
-                    nc.scalar.copy(dst[:, :LAST_SCALAR_M], src[:, :LAST_SCALAR_M])
-                    nc.vector.tensor_copy(dst[:, LAST_SCALAR_M:], src[:, LAST_SCALAR_M:])
-                else:
-                    nc.scalar.copy(dst, src)
-                cols = slice(c * HALF_M, (c + 1) * HALF_M)
-                for t in range(PACK):
-                    nc.vector.quantize_mx(
-                        out=w1_codes[g][:, t, cols].bitcast(FP8X4),
-                        scales=w1_planes[g][:, t, cols],
-                        in_=dealt[:, t].rearrange("p m j -> p (m j)"),
-                    )
+        def deal_w1(g):
+            dealt = keep.tile([P, PACK, P, PACK], BF16, name=f"dealt{g}", tag=f"dealt{g}", align_bytes=64)
+            src = w1_raw[g][:].rearrange("p j (m t) -> p m j t", t=PACK)
+            dst = dealt[:].rearrange("p t m j -> p m j t")
+            split = SCALAR_M[g]
+            nc.scalar.copy(dst[:, :split], src[:, :split])
+            nc.vector.tensor_copy(dst[:, split:], src[:, split:])
+            return dealt
+
+        def quantise_w1(g, dealt):
+            nc.vector.quantize_mx(
+                out=w1_codes[g][:].rearrange("p t m -> p (t m)").bitcast(FP8X4),
+                scales=w1_planes[g][:].rearrange("p t m -> p (t m)"),
+                in_=dealt[:].rearrange("p t m j -> p (t m j)"),
+            )
 
         h_banks = [psum.tile([P, PACK, CHUNK], F32, name=f"h_bank{u}") for u in range(CHUNKS)]
 
@@ -121,28 +125,33 @@ def tile_picked_modgate_mlpsilu_p_kernel(tc, x_words, x_scales, gate, w1, w2_wor
                     out=h_banks[u][:, t, :],
                     lhsT=w1_codes[g][:, t, :].bitcast(FP8X4),
                     lhsT_scale=w1_planes[g][:, t, :],
-                    rhs=words[:, tokens].bitcast(FP8X4),
+                    rhs=words.bitcast(FP8X4),
                     rhs_scale=picked_planes[4 * g :, tokens],
                     start=(g == 0 and t == 0),
                     stop=(g == PASSES - 1 and t == PACK - 1),
                 )
 
-        quantise_w1(0)
-        for u in range(CHUNKS):
-            first_product(u, 0, picked0)
-        quantise_w1(1)
-
         entries = [offsets[:, u * LIST_COLS : (u + 1) * LIST_COLS] for u in range(CHUNKS)]
-        picked1 = keep.tile([P, S], U32, name="picked1", tag="dealt1", align_bytes=64)
-        for u in range(CHUNKS):
-            nc.vector.tensor_copy(
-                picked1[:, u * CHUNK : (u + 1) * CHUNK], x_table[1][:].bitcast(U32).indirect(entries[u])
-            )
-        scores_first = keep.tile([P, CHUNK], F32, name="scores_first", tag="x_table1", align_bytes=64)
-        nc.vector.tensor_copy(scores_first[:], gate_table[:].indirect(entries[0]))
 
-        for u in range(CHUNKS):
-            first_product(u, 1, picked1)
+        def pick_words(g, u, words):
+            nc.vector.tensor_copy(words, x_table[g][:].bitcast(U32).indirect(entries[u]))
+
+        dealt = [deal_w1(g) for g in range(PASSES)]
+        quantise_w1(0, dealt[0])
+        picked_early = keep.tile([P, EARLY, CHUNK], U32, name="picked_early", tag="dealt0", align_bytes=64)
+        for u in range(EARLY):
+            pick_words(0, u, picked_early[:, u, :])
+            first_product(u, 0, picked_early[:, u, :])
+        quantise_w1(1, dealt[1])
+        late = [(g, u) for u in range(CHUNKS) for g in range(PASSES) if g > 0 or u >= EARLY]
+        picked_late = keep.tile([P, len(late), CHUNK], U32, name="picked_late", tag="dealt1", align_bytes=64)
+        for place, (g, u) in enumerate(late):
+            pick_words(g, u, picked_late[:, place, :])
+
+        def products(u):
+            for place, (g, v) in enumerate(late):
+                if v == u:
+                    first_product(u, g, picked_late[:, place, :])
             h = keep.tile([P, CHUNK, PACK], BF16, name=f"h{u}", tag=f"h{u}", align_bytes=64)
             nc.scalar.activation(h[:], h_banks[u][:].rearrange("p t n -> p n t"), SILU)
             h_codes = keep.tile([P, CHUNK], U32, name=f"h_codes{u}", align_bytes=64)
@@ -150,10 +159,7 @@ def tile_picked_modgate_mlpsilu_p_kernel(tc, x_words, x_scales, gate, w1, w2_wor
             nc.vector.quantize_mx(
                 out=h_codes[:].bitcast(FP8X4), scales=h_plane[:], in_=h[:].rearrange("p n t -> p (n t)")
             )
-            if u == 0:
-                scores_rest = keep.tile([P, S - CHUNK], F32, name="scores_rest", tag="h0", align_bytes=64)
-                nc.vector.tensor_copy(scores_rest[:], gate_table[:].indirect(offsets[:, LIST_COLS:]))
-            y_bank = psum.tile([P, CHUNK], F32, name=f"y_bank{u}")
+            y_bank = psum.tile([P, CHUNK], F32, name=f"y_bank{u}", tag=f"y_bank{u}")
             nc.tensor.matmul_mx(
                 out=y_bank[:],
                 lhsT=w2_codes[:].bitcast(FP8X4),
@@ -163,12 +169,20 @@ def tile_picked_modgate_mlpsilu_p_kernel(tc, x_words, x_scales, gate, w1, w2_wor
                 start=True,
                 stop=True,
             )
+            return y_bank
+
+        def put_back(u, y_bank):
             y = keep.tile([P, CHUNK], F32, name=f"y{u}", align_bytes=64)
             if u + 2 < CHUNKS:
                 nc.scalar.activation(y[:], y_bank[:], IDENTITY, bias=zero_bias[u][:])
             else:
                 nc.scalar.copy(y[:], y_bank[:])
-            scores = scores_first[:] if u == 0 else scores_rest[:, (u - 1) * CHUNK : u * CHUNK]
-            nc.vector.tensor_tensor(window[:].indirect(entries[u]), y[:], scores, MULT)
+            nc.vector.tensor_tensor(window[:].indirect(entries[u]), y[:], scores[:, u * CHUNK : (u + 1) * CHUNK], MULT)
+
+        y_banks = [products(0), products(1)]
+        for u in range(CHUNKS):
+            put_back(u, y_banks[u])
+            if u + 2 < CHUNKS:
+                y_banks.append(products(u + 2))
 
         nc.sync.dma_start(out, window[:])

@@ -1,7 +1,6 @@
 from contextlib import ExitStack
 
 import concourse.mybir as mybir
-from concourse.masks import make_identity
 
 K, T, S, H, N = 1024, 1024, 512, 512, 128
 FLOPS = 2 * S * H * (K + N)
@@ -14,19 +13,17 @@ U16 = mybir.dt.uint16
 U8 = mybir.dt.uint8
 FP8X4 = mybir.dt.float8_e4m3fn_x4
 SILU = mybir.ActivationFunctionType.Silu
-IDENTITY = mybir.ActivationFunctionType.Identity
 MULT = mybir.AluOpType.mult
 
 P = 128
 PACK = 4
 PASSES = K // (P * PACK)
+HALVES = 2
+HALF_M = P // HALVES
 CHUNK = 128
 CHUNKS = S // CHUNK
 LIST_COLS = CHUNK // 16
-SCALAR_M = [84, 72]
-EARLY = 2
-GATE_COLS = T // P
-PER_BANK = 4
+LAST_SCALAR_M = 24
 
 
 def tile_picked_modgate_mlpsilu_p_kernel(tc, x_words, x_scales, gate, w1, w2_words, w2_scales, offs, out):
@@ -35,43 +32,41 @@ def tile_picked_modgate_mlpsilu_p_kernel(tc, x_words, x_scales, gate, w1, w2_wor
         keep = ctx.enter_context(tc.tile_pool(name="keep", bufs=1))
         psum = ctx.enter_context(tc.psum_pool(name="psum", bufs=1))
 
-        x_planes = keep.tile([P, T], U8, name="x_planes", align_bytes=64)
+        x_planes = keep.tile([P, T], U8, name="x_planes", tag="x_planes", align_bytes=64)
         nc.gpsimd.memset(x_planes[:].bitcast(I32), 0)
         for q in range(4):
             nc.scalar.dma_start(
                 x_planes[32 * q : 32 * q + 4 * PASSES, :].bitcast(I32),
                 x_scales[:, 4 * q : 4 * q + 4, :].bitcast(I32),
             )
-        warm = keep.tile([P, 1], F32, name="warm")
+        warm_in = keep.tile([P, 1], F32, name="warm_in")
         warm_out = keep.tile([P, 1], F32, name="warm_out")
-        nc.gpsimd.memset(warm[:], 0.0)
-        nc.scalar.activation(warm_out[:], warm[:], SILU)
+        nc.gpsimd.memset(warm_in[:], 0.0)
+        nc.scalar.activation(warm_out[:], warm_in[:], SILU)
 
-        x_table = [keep.tile([P, T], I32, name=f"x_table{g}", align_bytes=64) for g in range(PASSES)]
-        w1_raw = [keep.tile([P, PACK, H], F32, name=f"w1_raw{g}", align_bytes=64) for g in range(PASSES)]
+        x_table = [
+            keep.tile([P, T], I32, name=f"x_table{g}", tag=f"x_table{g}", align_bytes=64) for g in range(PASSES)
+        ]
+        w1_raw = [
+            [keep.tile([P, PACK, H // HALVES], F32, name=f"w1_raw{g}{c}", align_bytes=64) for c in range(HALVES)]
+            for g in range(PASSES)
+        ]
 
         def load_x(g):
             nc.sync.dma_start(x_table[g][:], x_words[g].rearrange("p n t -> p (n t)").bitcast(I32))
 
-        gate_row = keep.tile([P, GATE_COLS], F32, name="gate_row", tag="dealt0", align_bytes=64)
-        nc.sync.dma_start(gate_row[:], gate[0].rearrange("(p c) -> p c", c=GATE_COLS))
+        load_x(0)
         offsets = keep.tile([P, S // 16], U16, name="offsets")
         nc.sync.dma_start(offsets[:], offs)
         for g in range(PASSES):
             rows = w1[g * P * PACK : (g + 1) * P * PACK, :].rearrange("(p j) h -> p j h", j=PACK)
-            nc.sync.dma_start(w1_raw[g][:], rows)
-        for g in range(PASSES):
-            load_x(g)
+            for c in range(HALVES):
+                nc.sync.dma_start(w1_raw[g][c][:], rows[:, :, c * (H // HALVES) : (c + 1) * (H // HALVES)])
+        load_x(1)
+        gate_table = keep.tile([P, T], F32, name="gate_table", align_bytes=64)
+        nc.sync.dma_start(gate_table[:], gate)
         w2_codes = keep.tile([P, N], I32, name="w2_codes", align_bytes=64)
         nc.sync.dma_start(w2_codes[:], w2_words[0].rearrange("p n t -> p (n t)").bitcast(I32))
-
-        identity = keep.tile([P, P], F32, name="identity", align_bytes=64)
-        make_identity(nc, identity[:])
-        zero_bias = [
-            keep.tile([P, 1], F32, name=f"zero_bias{u}", tag=f"h{u + 2}", align_bytes=64) for u in range(CHUNKS - 2)
-        ]
-        for zero in zero_bias:
-            nc.gpsimd.memset(zero[:], 0.0)
         w2_plane = keep.tile([P, N], U8, name="w2_plane", align_bytes=64)
         nc.gpsimd.memset(w2_plane[:].bitcast(I32), 0)
         for q in range(4):
@@ -83,38 +78,17 @@ def tile_picked_modgate_mlpsilu_p_kernel(tc, x_words, x_scales, gate, w1, w2_wor
         window = keep.tile([P, T], F32, name="window", align_bytes=64)
         nc.vector.memset(window[:], 0.0)
 
-        gate_table = keep.tile([P, T], F32, name="gate_table", tag="dealt1", align_bytes=64)
-        gate_view = gate_table[:].rearrange("p (n c) -> p n c", c=GATE_COLS)
-        for b in range(GATE_COLS // PER_BANK):
-            spread = psum.tile([P, PER_BANK, P], F32, name=f"spread{b}", tag=f"y_bank{b}")
-            for c in range(PER_BANK):
-                col = b * PER_BANK + c
-                nc.tensor.transpose(spread[:, c, :], gate_row[:, col : col + 1].to_broadcast([P, P]), identity[:])
-            nc.scalar.copy(gate_view[:, :, b * PER_BANK : (b + 1) * PER_BANK], spread[:].rearrange("p c n -> p n c"))
-
-        picked_planes = keep.tile([P, S], U8, name="picked_planes", align_bytes=64)
+        picked0 = keep.tile([P, S], U32, name="picked0", align_bytes=64)
+        nc.vector.tensor_copy(picked0[:], x_table[0][:].bitcast(U32).indirect(offsets[:]))
+        picked_planes = keep.tile([P, S], U8, name="picked_planes", tag="x_table0", align_bytes=64)
         nc.vector.tensor_copy(picked_planes[:], x_planes[:].indirect(offsets[:]))
-        scores = keep.tile([P, S], F32, name="scores", align_bytes=64)
-        nc.vector.tensor_copy(scores[:], gate_table[:].indirect(offsets[:]))
 
         w1_codes = [keep.tile([P, PACK, P], U32, name=f"w1_codes{g}", align_bytes=64) for g in range(PASSES)]
         w1_planes = [keep.tile([P, PACK, P], U8, name=f"w1_planes{g}", align_bytes=64) for g in range(PASSES)]
 
-        def deal_w1(g):
-            dealt = keep.tile([P, PACK, P, PACK], BF16, name=f"dealt{g}", tag=f"dealt{g}", align_bytes=64)
-            src = w1_raw[g][:].rearrange("p j (m t) -> p m j t", t=PACK)
-            dst = dealt[:].rearrange("p t m j -> p m j t")
-            split = SCALAR_M[g]
-            nc.scalar.copy(dst[:, :split], src[:, :split])
-            nc.vector.tensor_copy(dst[:, split:], src[:, split:])
-            return dealt
-
-        def quantise_w1(g, dealt):
-            nc.vector.quantize_mx(
-                out=w1_codes[g][:].rearrange("p t m -> p (t m)").bitcast(FP8X4),
-                scales=w1_planes[g][:].rearrange("p t m -> p (t m)"),
-                in_=dealt[:].rearrange("p t m j -> p (t m j)"),
-            )
+        def deal_views(g, c, dealt):
+            src = w1_raw[g][c][:].rearrange("p j (m t) -> p m j t", t=PACK)
+            return dealt.rearrange("p t m j -> p m j t"), src
 
         h_banks = [psum.tile([P, PACK, CHUNK], F32, name=f"h_bank{u}") for u in range(CHUNKS)]
 
@@ -125,33 +99,55 @@ def tile_picked_modgate_mlpsilu_p_kernel(tc, x_words, x_scales, gate, w1, w2_wor
                     out=h_banks[u][:, t, :],
                     lhsT=w1_codes[g][:, t, :].bitcast(FP8X4),
                     lhsT_scale=w1_planes[g][:, t, :],
-                    rhs=words.bitcast(FP8X4),
+                    rhs=words[:, tokens].bitcast(FP8X4),
                     rhs_scale=picked_planes[4 * g :, tokens],
                     start=(g == 0 and t == 0),
                     stop=(g == PASSES - 1 and t == PACK - 1),
                 )
 
+        dealt0 = keep.tile([P, PACK, P, PACK], BF16, name="dealt0", tag="dealt0", align_bytes=64)
+        for c in range(HALVES):
+            nc.scalar.copy(*deal_views(0, c, dealt0[:, :, c * HALF_M : (c + 1) * HALF_M, :]))
+        nc.vector.quantize_mx(
+            out=w1_codes[0][:].rearrange("p t m -> p (t m)").bitcast(FP8X4),
+            scales=w1_planes[0][:].rearrange("p t m -> p (t m)"),
+            in_=dealt0[:].rearrange("p t m j -> p (t m j)"),
+        )
+        for u in range(CHUNKS):
+            first_product(u, 0, picked0)
+
+        for c in range(HALVES):
+            dealt = keep.tile(
+                [P, PACK, HALF_M, PACK], BF16, name=f"dealt1{c}", tag=("dealt10", "dealt0")[c], align_bytes=64
+            )
+            dst, src = deal_views(1, c, dealt[:])
+            if c == HALVES - 1:
+                nc.scalar.copy(dst[:, :LAST_SCALAR_M], src[:, :LAST_SCALAR_M])
+                nc.vector.tensor_copy(dst[:, LAST_SCALAR_M:], src[:, LAST_SCALAR_M:])
+            else:
+                nc.scalar.copy(dst, src)
+            cols = slice(c * HALF_M, (c + 1) * HALF_M)
+            for t in range(PACK):
+                nc.vector.quantize_mx(
+                    out=w1_codes[1][:, t, cols].bitcast(FP8X4),
+                    scales=w1_planes[1][:, t, cols],
+                    in_=dealt[:, t].rearrange("p m j -> p (m j)"),
+                )
+
         entries = [offsets[:, u * LIST_COLS : (u + 1) * LIST_COLS] for u in range(CHUNKS)]
+        picked1 = keep.tile([P, S], U32, name="picked1", tag="dealt0", align_bytes=64)
+        for u in range(CHUNKS):
+            nc.vector.tensor_copy(
+                picked1[:, u * CHUNK : (u + 1) * CHUNK], x_table[1][:].bitcast(U32).indirect(entries[u])
+            )
 
-        def pick_words(g, u, words):
-            nc.vector.tensor_copy(words, x_table[g][:].bitcast(U32).indirect(entries[u]))
-
-        dealt = [deal_w1(g) for g in range(PASSES)]
-        quantise_w1(0, dealt[0])
-        picked_early = keep.tile([P, EARLY, CHUNK], U32, name="picked_early", tag="dealt0", align_bytes=64)
-        for u in range(EARLY):
-            pick_words(0, u, picked_early[:, u, :])
-            first_product(u, 0, picked_early[:, u, :])
-        quantise_w1(1, dealt[1])
-        late = [(g, u) for u in range(CHUNKS) for g in range(PASSES) if g > 0 or u >= EARLY]
-        picked_late = keep.tile([P, len(late), CHUNK], U32, name="picked_late", tag="dealt1", align_bytes=64)
-        for place, (g, u) in enumerate(late):
-            pick_words(g, u, picked_late[:, place, :])
+        def pick_scores(first, last, tag):
+            scores = keep.tile([P, (last - first) * CHUNK], F32, name=f"scores{first}", tag=tag, align_bytes=64)
+            nc.vector.tensor_copy(scores[:], gate_table[:].indirect(offsets[:, first * LIST_COLS : last * LIST_COLS]))
+            return scores
 
         def products(u):
-            for place, (g, v) in enumerate(late):
-                if v == u:
-                    first_product(u, g, picked_late[:, place, :])
+            first_product(u, 1, picked1)
             h = keep.tile([P, CHUNK, PACK], BF16, name=f"h{u}", tag=f"h{u}", align_bytes=64)
             nc.scalar.activation(h[:], h_banks[u][:].rearrange("p t n -> p n t"), SILU)
             h_codes = keep.tile([P, CHUNK], U32, name=f"h_codes{u}", align_bytes=64)
@@ -159,7 +155,7 @@ def tile_picked_modgate_mlpsilu_p_kernel(tc, x_words, x_scales, gate, w1, w2_wor
             nc.vector.quantize_mx(
                 out=h_codes[:].bitcast(FP8X4), scales=h_plane[:], in_=h[:].rearrange("p n t -> p (n t)")
             )
-            y_bank = psum.tile([P, CHUNK], F32, name=f"y_bank{u}", tag=f"y_bank{u}")
+            y_bank = psum.tile([P, CHUNK], F32, name=f"y_bank{u}")
             nc.tensor.matmul_mx(
                 out=y_bank[:],
                 lhsT=w2_codes[:].bitcast(FP8X4),
@@ -171,18 +167,23 @@ def tile_picked_modgate_mlpsilu_p_kernel(tc, x_words, x_scales, gate, w1, w2_wor
             )
             return y_bank
 
-        def put_back(u, y_bank):
-            y = keep.tile([P, CHUNK], F32, name=f"y{u}", align_bytes=64)
-            if u + 2 < CHUNKS:
-                nc.scalar.activation(y[:], y_bank[:], IDENTITY, bias=zero_bias[u][:])
-            else:
-                nc.scalar.copy(y[:], y_bank[:])
-            nc.vector.tensor_tensor(window[:].indirect(entries[u]), y[:], scores[:, u * CHUNK : (u + 1) * CHUNK], MULT)
+        y = keep.tile([P, S], F32, name="y", align_bytes=64)
 
-        y_banks = [products(0), products(1)]
-        for u in range(CHUNKS):
-            put_back(u, y_banks[u])
-            if u + 2 < CHUNKS:
-                y_banks.append(products(u + 2))
+        def put_back(first, last, scores):
+            for u in range(first, last):
+                nc.scalar.copy(y[:, u * CHUNK : (u + 1) * CHUNK], y_banks[u][:])
+            nc.vector.tensor_tensor(
+                window[:].indirect(offsets[:, first * LIST_COLS : last * LIST_COLS]),
+                y[:, first * CHUNK : last * CHUNK],
+                scores[:],
+                MULT,
+            )
+
+        scores_first = pick_scores(0, 1, "x_table1")
+        y_banks = [products(0)]
+        scores_rest = pick_scores(1, CHUNKS, "h0")
+        y_banks.extend(products(u) for u in range(1, CHUNKS))
+        put_back(0, 1, scores_first)
+        put_back(1, CHUNKS, scores_rest)
 
         nc.sync.dma_start(out, window[:])

@@ -23,72 +23,96 @@ HALF_M = P // HALVES
 CHUNK = 128
 CHUNKS = S // CHUNK
 LIST_COLS = CHUNK // 16
-LAST_SCALAR_M = 24
+SCALAR_M = ((64, 24), (64, 24))
 
 
 def tile_picked_modgate_mlpsilu_p_kernel(tc, x_words, x_scales, gate, w1, w2_words, w2_scales, offs, out):
     nc = tc.nc
     with ExitStack() as ctx:
         keep = ctx.enter_context(tc.tile_pool(name="keep", bufs=1))
+        late = ctx.enter_context(tc.tile_pool(name="late", bufs=1))
         psum = ctx.enter_context(tc.psum_pool(name="psum", bufs=1))
 
-        x_planes = keep.tile([P, T], U8, name="x_planes", tag="x_planes", align_bytes=64)
+        x_planes = keep.tile([P, T], U8, name="x_planes", align_bytes=64)
         nc.gpsimd.memset(x_planes[:].bitcast(I32), 0)
-        for q in range(4):
-            nc.scalar.dma_start(
-                x_planes[32 * q : 32 * q + 4 * PASSES, :].bitcast(I32),
-                x_scales[:, 4 * q : 4 * q + 4, :].bitcast(I32),
-            )
-        warm_in = keep.tile([P, 1], F32, name="warm_in")
+        warm_in = late.tile([P, 5 * T + N + N // 4], F32, name="warm_in", offset=0, align_bytes=64)
         warm_out = keep.tile([P, 1], F32, name="warm_out")
-        nc.gpsimd.memset(warm_in[:], 0.0)
-        nc.scalar.activation(warm_out[:], warm_in[:], SILU)
+        nc.gpsimd.memset(warm_in[:, :1], 0.0)
+        nc.scalar.activation(warm_out[:], warm_in[:, :1], SILU)
 
         x_table = [
-            keep.tile([P, T], I32, name=f"x_table{g}", tag=f"x_table{g}", align_bytes=64) for g in range(PASSES)
+            keep.tile([P, T], I32, name="x_table0", align_bytes=64),
+            late.tile([P, T], I32, name="x_table1", offset=0, align_bytes=64),
         ]
         w1_raw = [
-            [keep.tile([P, PACK, H // HALVES], F32, name=f"w1_raw{g}{c}", align_bytes=64) for c in range(HALVES)]
-            for g in range(PASSES)
+            [
+                keep.tile([P, PACK, H // HALVES], F32, name="w1_raw00", align_bytes=64),
+                late.tile([P, PACK, H // HALVES], F32, name="w1_raw01", offset=4 * T * 4, align_bytes=64),
+            ],
+            [
+                late.tile([P, PACK, H // HALVES], F32, name=f"w1_raw1{c}", offset=4 * T * (1 + c), align_bytes=64)
+                for c in range(HALVES)
+            ],
         ]
+        offsets = keep.tile([P, S // 16], U16, name="offsets")
 
         def load_x(g):
             nc.sync.dma_start(x_table[g][:], x_words[g].rearrange("p n t -> p (n t)").bitcast(I32))
 
-        load_x(0)
-        offsets = keep.tile([P, S // 16], U16, name="offsets")
-        nc.sync.dma_start(offsets[:], offs)
-        for g in range(PASSES):
+        def load_w1(g, c):
             rows = w1[g * P * PACK : (g + 1) * P * PACK, :].rearrange("(p j) h -> p j h", j=PACK)
-            for c in range(HALVES):
-                nc.sync.dma_start(w1_raw[g][c][:], rows[:, :, c * (H // HALVES) : (c + 1) * (H // HALVES)])
-        load_x(1)
-        gate_table = keep.tile([P, T], F32, name="gate_table", align_bytes=64)
-        nc.sync.dma_start(gate_table[:], gate)
-        w2_codes = keep.tile([P, N], I32, name="w2_codes", align_bytes=64)
+            nc.sync.dma_start(w1_raw[g][c][:], rows[:, :, c * (H // HALVES) : (c + 1) * (H // HALVES)])
+
+        load_x(0)
+        nc.sync.dma_start(offsets[:], offs)
+        load_w1(0, 0)
+        for q in range(4):
+            nc.sync.dma_start(
+                x_planes[32 * q : 32 * q + 4 * PASSES, :].bitcast(I32),
+                x_scales[:, 4 * q : 4 * q + 4, :].bitcast(I32),
+            )
+        load_w1(0, 1)
+        load_w1(1, 0)
+        load_w1(1, 1)
+        w2_codes = late.tile([P, N], I32, name="w2_codes", offset=4 * T * 5, align_bytes=64)
         nc.sync.dma_start(w2_codes[:], w2_words[0].rearrange("p n t -> p (n t)").bitcast(I32))
-        w2_plane = keep.tile([P, N], U8, name="w2_plane", align_bytes=64)
+        w2_plane = late.tile([P, N], U8, name="w2_plane", offset=4 * (T * 5 + N), align_bytes=64)
         nc.gpsimd.memset(w2_plane[:].bitcast(I32), 0)
         for q in range(4):
             nc.sync.dma_start(
                 w2_plane[32 * q : 32 * q + 4, :].bitcast(I32),
                 w2_scales[0, 4 * q : 4 * q + 4, :].bitcast(I32),
             )
+        load_x(1)
+        gate_table = late.tile([P, T], F32, name="gate_table", offset=4 * T * 3, align_bytes=64)
+        nc.sync.dma_start(gate_table[:], gate)
 
         window = keep.tile([P, T], F32, name="window", align_bytes=64)
         nc.vector.memset(window[:], 0.0)
 
-        picked0 = keep.tile([P, S], U32, name="picked0", align_bytes=64)
-        nc.vector.tensor_copy(picked0[:], x_table[0][:].bitcast(U32).indirect(offsets[:]))
-        picked_planes = keep.tile([P, S], U8, name="picked_planes", tag="x_table0", align_bytes=64)
+        def entries(first, last):
+            return offsets[:, first * LIST_COLS : last * LIST_COLS]
+
+        def pick_words(g, first, last, tag):
+            words = keep.tile([P, (last - first) * CHUNK], U32, name=f"picked{g}{first}", tag=tag, align_bytes=64)
+            nc.vector.tensor_copy(words[:], x_table[g][:].bitcast(U32).indirect(entries(first, last)))
+            return [words[:, v * CHUNK : (v + 1) * CHUNK] for v in range(last - first)]
+
+        picked0 = pick_words(0, 0, CHUNKS, "picked0")
+        picked_planes = keep.tile([P, S], U8, name="picked_planes", align_bytes=64)
         nc.vector.tensor_copy(picked_planes[:], x_planes[:].indirect(offsets[:]))
 
         w1_codes = [keep.tile([P, PACK, P], U32, name=f"w1_codes{g}", align_bytes=64) for g in range(PASSES)]
         w1_planes = [keep.tile([P, PACK, P], U8, name=f"w1_planes{g}", align_bytes=64) for g in range(PASSES)]
 
-        def deal_views(g, c, dealt):
+        def deal(g, c, dealt):
             src = w1_raw[g][c][:].rearrange("p j (m t) -> p m j t", t=PACK)
-            return dealt.rearrange("p t m j -> p m j t"), src
+            dst = dealt.rearrange("p t m j -> p m j t")
+            split = SCALAR_M[g][c]
+            if split > 0:
+                nc.scalar.copy(dst[:, :split], src[:, :split])
+            if split < HALF_M:
+                nc.vector.tensor_copy(dst[:, split:], src[:, split:])
 
         h_banks = [psum.tile([P, PACK, CHUNK], F32, name=f"h_bank{u}") for u in range(CHUNKS)]
 
@@ -99,7 +123,7 @@ def tile_picked_modgate_mlpsilu_p_kernel(tc, x_words, x_scales, gate, w1, w2_wor
                     out=h_banks[u][:, t, :],
                     lhsT=w1_codes[g][:, t, :].bitcast(FP8X4),
                     lhsT_scale=w1_planes[g][:, t, :],
-                    rhs=words[:, tokens].bitcast(FP8X4),
+                    rhs=words.bitcast(FP8X4),
                     rhs_scale=picked_planes[4 * g :, tokens],
                     start=(g == 0 and t == 0),
                     stop=(g == PASSES - 1 and t == PACK - 1),
@@ -107,25 +131,18 @@ def tile_picked_modgate_mlpsilu_p_kernel(tc, x_words, x_scales, gate, w1, w2_wor
 
         dealt0 = keep.tile([P, PACK, P, PACK], BF16, name="dealt0", tag="dealt0", align_bytes=64)
         for c in range(HALVES):
-            nc.scalar.copy(*deal_views(0, c, dealt0[:, :, c * HALF_M : (c + 1) * HALF_M, :]))
+            deal(0, c, dealt0[:, :, c * HALF_M : (c + 1) * HALF_M, :])
         nc.vector.quantize_mx(
             out=w1_codes[0][:].rearrange("p t m -> p (t m)").bitcast(FP8X4),
             scales=w1_planes[0][:].rearrange("p t m -> p (t m)"),
             in_=dealt0[:].rearrange("p t m j -> p (t m j)"),
         )
         for u in range(CHUNKS):
-            first_product(u, 0, picked0)
+            first_product(u, 0, picked0[u])
 
         for c in range(HALVES):
-            dealt = keep.tile(
-                [P, PACK, HALF_M, PACK], BF16, name=f"dealt1{c}", tag=("dealt10", "dealt0")[c], align_bytes=64
-            )
-            dst, src = deal_views(1, c, dealt[:])
-            if c == HALVES - 1:
-                nc.scalar.copy(dst[:, :LAST_SCALAR_M], src[:, :LAST_SCALAR_M])
-                nc.vector.tensor_copy(dst[:, LAST_SCALAR_M:], src[:, LAST_SCALAR_M:])
-            else:
-                nc.scalar.copy(dst, src)
+            dealt = keep.tile([P, PACK, HALF_M, PACK], BF16, name=f"dealt1{c}", tag=f"dealt1{c}", align_bytes=64)
+            deal(1, c, dealt[:])
             cols = slice(c * HALF_M, (c + 1) * HALF_M)
             for t in range(PACK):
                 nc.vector.quantize_mx(
@@ -134,22 +151,18 @@ def tile_picked_modgate_mlpsilu_p_kernel(tc, x_words, x_scales, gate, w1, w2_wor
                     in_=dealt[:, t].rearrange("p m j -> p (m j)"),
                 )
 
-        entries = [offsets[:, u * LIST_COLS : (u + 1) * LIST_COLS] for u in range(CHUNKS)]
-        picked1 = keep.tile([P, S], U32, name="picked1", tag="dealt0", align_bytes=64)
-        for u in range(CHUNKS):
-            nc.vector.tensor_copy(
-                picked1[:, u * CHUNK : (u + 1) * CHUNK], x_table[1][:].bitcast(U32).indirect(entries[u])
-            )
-
         def pick_scores(first, last, tag):
             scores = keep.tile([P, (last - first) * CHUNK], F32, name=f"scores{first}", tag=tag, align_bytes=64)
-            nc.vector.tensor_copy(scores[:], gate_table[:].indirect(offsets[:, first * LIST_COLS : last * LIST_COLS]))
+            nc.vector.tensor_copy(scores[:], gate_table[:].indirect(entries(first, last)))
             return scores
 
-        def products(u):
-            first_product(u, 1, picked1)
-            h = keep.tile([P, CHUNK, PACK], BF16, name=f"h{u}", tag=f"h{u}", align_bytes=64)
+        def hidden(u, words, tag):
+            first_product(u, 1, words)
+            h = keep.tile([P, CHUNK, PACK], BF16, name=f"h{u}", tag=tag, align_bytes=64)
             nc.scalar.activation(h[:], h_banks[u][:].rearrange("p t n -> p n t"), SILU)
+            return h
+
+        def second_product(u, h):
             h_codes = keep.tile([P, CHUNK], U32, name=f"h_codes{u}", align_bytes=64)
             h_plane = keep.tile([P, CHUNK], U8, name=f"h_plane{u}", align_bytes=64)
             nc.vector.quantize_mx(
@@ -169,21 +182,27 @@ def tile_picked_modgate_mlpsilu_p_kernel(tc, x_words, x_scales, gate, w1, w2_wor
 
         y = keep.tile([P, S], F32, name="y", align_bytes=64)
 
+        def fetch(u, y_bank):
+            nc.scalar.copy(y[:, u * CHUNK : (u + 1) * CHUNK], y_bank[:])
+
         def put_back(first, last, scores):
-            for u in range(first, last):
-                nc.scalar.copy(y[:, u * CHUNK : (u + 1) * CHUNK], y_banks[u][:])
             nc.vector.tensor_tensor(
-                window[:].indirect(offsets[:, first * LIST_COLS : last * LIST_COLS]),
-                y[:, first * CHUNK : last * CHUNK],
-                scores[:],
-                MULT,
+                window[:].indirect(entries(first, last)), y[:, first * CHUNK : last * CHUNK], scores, MULT
             )
 
-        scores_first = pick_scores(0, 1, "x_table1")
-        y_banks = [products(0)]
-        scores_rest = pick_scores(1, CHUNKS, "h0")
-        y_banks.extend(products(u) for u in range(1, CHUNKS))
-        put_back(0, 1, scores_first)
-        put_back(1, CHUNKS, scores_rest)
+        picked1 = pick_words(1, 0, 1, "picked10") + pick_words(1, 1, 2, "dealt11") + pick_words(1, 2, 4, "dealt10")
+        h = [hidden(u, picked1[u], f"h{u}") for u in range(CHUNKS)]
+        scores_first = pick_scores(0, 2, "scores0")
+        y_banks = [second_product(0, h[0])]
+        scores_rest = pick_scores(2, CHUNKS, "h0")
+        y_banks.append(second_product(1, h[1]))
+        nc.vector.tensor_tensor(y[:, :CHUNK], y_banks[0][:], scores_first[:, :CHUNK], MULT)
+        nc.vector.tensor_copy(window[:].indirect(entries(0, 1)), y[:, :CHUNK])
+        y_banks.extend(second_product(u, h[u]) for u in (2, 3))
+        fetch(1, y_banks[1])
+        put_back(1, 2, scores_first[:, CHUNK:])
+        fetch(2, y_banks[2])
+        fetch(3, y_banks[3])
+        put_back(2, 4, scores_rest[:])
 
         nc.sync.dma_start(out, window[:])

@@ -74,6 +74,9 @@ def tile_picked_modgate_mlpsilu_p_kernel(tc, x_words, x_scales, gate, w1, w2_wor
         load_w1(0, 1)
         load_w1(1, 0)
         load_w1(1, 1)
+        load_x(1)
+        gate_table = late.tile([P, T], F32, name="gate_table", offset=4 * T * 3, align_bytes=64)
+        nc.sync.dma_start(gate_table[:], gate)
         w2_codes = late.tile([P, N], I32, name="w2_codes", offset=4 * T * 5, align_bytes=64)
         nc.sync.dma_start(w2_codes[:], w2_words[0].rearrange("p n t -> p (n t)").bitcast(I32))
         w2_plane = late.tile([P, N], U8, name="w2_plane", offset=4 * (T * 5 + N), align_bytes=64)
@@ -83,9 +86,6 @@ def tile_picked_modgate_mlpsilu_p_kernel(tc, x_words, x_scales, gate, w1, w2_wor
                 w2_plane[32 * q : 32 * q + 4, :].bitcast(I32),
                 w2_scales[0, 4 * q : 4 * q + 4, :].bitcast(I32),
             )
-        load_x(1)
-        gate_table = late.tile([P, T], F32, name="gate_table", offset=4 * T * 3, align_bytes=64)
-        nc.sync.dma_start(gate_table[:], gate)
 
         window = keep.tile([P, T], F32, name="window", align_bytes=64)
         nc.vector.memset(window[:], 0.0)
@@ -112,7 +112,10 @@ def tile_picked_modgate_mlpsilu_p_kernel(tc, x_words, x_scales, gate, w1, w2_wor
             if split > 0:
                 nc.scalar.copy(dst[:, :split], src[:, :split])
             if split < HALF_M:
-                nc.vector.tensor_copy(dst[:, split:], src[:, split:])
+                nc.vector.tensor_copy(
+                    dealt.rearrange("p (a t) m j -> p a m j t", a=2)[:, :, split:],
+                    w1_raw[g][c][:].rearrange("p j (m a t) -> p a m j t", a=2, t=2)[:, :, split:],
+                )
 
         h_banks = [psum.tile([P, PACK, CHUNK], F32, name=f"h_bank{u}") for u in range(CHUNKS)]
 
@@ -192,17 +195,14 @@ def tile_picked_modgate_mlpsilu_p_kernel(tc, x_words, x_scales, gate, w1, w2_wor
 
         picked1 = pick_words(1, 0, 1, "picked10") + pick_words(1, 1, 2, "dealt11") + pick_words(1, 2, 4, "dealt10")
         h = [hidden(u, picked1[u], f"h{u}") for u in range(CHUNKS)]
-        scores_first = pick_scores(0, 2, "scores0")
+        scores_first = pick_scores(0, 1, "scores0")
         y_banks = [second_product(0, h[0])]
-        scores_rest = pick_scores(2, CHUNKS, "h0")
-        y_banks.append(second_product(1, h[1]))
-        nc.vector.tensor_tensor(y[:, :CHUNK], y_banks[0][:], scores_first[:, :CHUNK], MULT)
-        nc.vector.tensor_copy(window[:].indirect(entries(0, 1)), y[:, :CHUNK])
-        y_banks.extend(second_product(u, h[u]) for u in (2, 3))
-        fetch(1, y_banks[1])
-        put_back(1, 2, scores_first[:, CHUNK:])
-        fetch(2, y_banks[2])
-        fetch(3, y_banks[3])
-        put_back(2, 4, scores_rest[:])
+        scores_rest = pick_scores(1, CHUNKS, "h0")
+        y_banks.extend(second_product(u, h[u]) for u in range(1, CHUNKS))
+        fetch(0, y_banks[0])
+        put_back(0, 1, scores_first[:])
+        for u in range(1, CHUNKS):
+            fetch(u, y_banks[u])
+        put_back(1, CHUNKS, scores_rest[:])
 
         nc.sync.dma_start(out, window[:])

@@ -18,70 +18,58 @@ MULT = mybir.AluOpType.mult
 P = 128
 PACK = 4
 PASSES = K // (P * PACK)
+QUADRANTS = 4
 HALVES = 2
 HALF_M = P // HALVES
 CHUNK = 128
 CHUNKS = S // CHUNK
 LIST_COLS = CHUNK // 16
-SCALAR_M = ((64, 24), (64, 24))
+SCALAR_M_PASS0 = 40
+SCALAR_M_PASS1 = (HALF_M, 24)
 
 
 def tile_picked_modgate_mlpsilu_p_kernel(tc, x_words, x_scales, gate, w1, w2_words, w2_scales, offs, out):
     nc = tc.nc
     with ExitStack() as ctx:
         keep = ctx.enter_context(tc.tile_pool(name="keep", bufs=1))
-        late = ctx.enter_context(tc.tile_pool(name="late", bufs=1))
         psum = ctx.enter_context(tc.psum_pool(name="psum", bufs=1))
 
         x_planes = keep.tile([P, T], U8, name="x_planes", align_bytes=64)
         nc.gpsimd.memset(x_planes[:].bitcast(I32), 0)
-        warm_in = late.tile([P, 5 * T + N + N // 4], F32, name="warm_in", offset=0, align_bytes=64)
-        warm_out = keep.tile([P, 1], F32, name="warm_out")
-        nc.gpsimd.memset(warm_in[:, :1], 0.0)
-        nc.scalar.activation(warm_out[:], warm_in[:, :1], SILU)
 
-        x_table = [
-            keep.tile([P, T], I32, name="x_table0", align_bytes=64),
-            late.tile([P, T], I32, name="x_table1", offset=0, align_bytes=64),
-        ]
-        w1_raw = [
-            [
-                keep.tile([P, PACK, H // HALVES], F32, name="w1_raw00", align_bytes=64),
-                late.tile([P, PACK, H // HALVES], F32, name="w1_raw01", offset=4 * T * 4, align_bytes=64),
-            ],
-            [
-                late.tile([P, PACK, H // HALVES], F32, name=f"w1_raw1{c}", offset=4 * T * (1 + c), align_bytes=64)
-                for c in range(HALVES)
-            ],
-        ]
+        warm_in = keep.tile([P, 1], F32, name="warm_in")
+        warm_out = keep.tile([P, 1], F32, name="warm_out")
+        nc.gpsimd.memset(warm_in[:], 0.0)
+        nc.scalar.activation(warm_out[:], warm_in[:], SILU)
+
+        x_table = [keep.tile([P, T], I32, name=f"x_table{g}", align_bytes=64) for g in range(PASSES)]
+        w1_raw0 = keep.tile([P, PACK, H], F32, name="w1_raw0", align_bytes=64)
+        w1_raw1 = [keep.tile([P, PACK, H // HALVES], F32, name=f"w1_raw1{c}", align_bytes=64) for c in range(HALVES)]
         offsets = keep.tile([P, S // 16], U16, name="offsets")
 
         def load_x(g):
             nc.sync.dma_start(x_table[g][:], x_words[g].rearrange("p n t -> p (n t)").bitcast(I32))
 
-        def load_w1(g, c):
-            rows = w1[g * P * PACK : (g + 1) * P * PACK, :].rearrange("(p j) h -> p j h", j=PACK)
-            nc.sync.dma_start(w1_raw[g][c][:], rows[:, :, c * (H // HALVES) : (c + 1) * (H // HALVES)])
+        w1_rows = [w1[g * P * PACK : (g + 1) * P * PACK, :].rearrange("(p j) h -> p j h", j=PACK) for g in range(PASSES)]
 
         load_x(0)
         nc.sync.dma_start(offsets[:], offs)
-        load_w1(0, 0)
-        for q in range(4):
+        for q in range(QUADRANTS):
             nc.sync.dma_start(
                 x_planes[32 * q : 32 * q + 4 * PASSES, :].bitcast(I32),
                 x_scales[:, 4 * q : 4 * q + 4, :].bitcast(I32),
             )
-        load_w1(0, 1)
-        load_w1(1, 0)
-        load_w1(1, 1)
+        nc.sync.dma_start(w1_raw0[:], w1_rows[0])
+        for c in range(HALVES):
+            nc.sync.dma_start(w1_raw1[c][:], w1_rows[1][:, :, c * (H // HALVES) : (c + 1) * (H // HALVES)])
         load_x(1)
-        gate_table = late.tile([P, T], F32, name="gate_table", offset=4 * T * 3, align_bytes=64)
+        gate_table = keep.tile([P, T], F32, name="gate_table", align_bytes=64)
         nc.sync.dma_start(gate_table[:], gate)
-        w2_codes = late.tile([P, N], I32, name="w2_codes", offset=4 * T * 5, align_bytes=64)
+        w2_codes = keep.tile([P, N], I32, name="w2_codes", align_bytes=64)
         nc.sync.dma_start(w2_codes[:], w2_words[0].rearrange("p n t -> p (n t)").bitcast(I32))
-        w2_plane = late.tile([P, N], U8, name="w2_plane", offset=4 * (T * 5 + N), align_bytes=64)
+        w2_plane = keep.tile([P, N], U8, name="w2_plane", align_bytes=64)
         nc.gpsimd.memset(w2_plane[:].bitcast(I32), 0)
-        for q in range(4):
+        for q in range(QUADRANTS):
             nc.sync.dma_start(
                 w2_plane[32 * q : 32 * q + 4, :].bitcast(I32),
                 w2_scales[0, 4 * q : 4 * q + 4, :].bitcast(I32),
@@ -105,16 +93,23 @@ def tile_picked_modgate_mlpsilu_p_kernel(tc, x_words, x_scales, gate, w1, w2_wor
         w1_codes = [keep.tile([P, PACK, P], U32, name=f"w1_codes{g}", align_bytes=64) for g in range(PASSES)]
         w1_planes = [keep.tile([P, PACK, P], U8, name=f"w1_planes{g}", align_bytes=64) for g in range(PASSES)]
 
-        def deal(g, c, dealt):
-            src = w1_raw[g][c][:].rearrange("p j (m t) -> p m j t", t=PACK)
-            dst = dealt.rearrange("p t m j -> p m j t")
-            split = SCALAR_M[g][c]
-            if split > 0:
-                nc.scalar.copy(dst[:, :split], src[:, :split])
-            if split < HALF_M:
+        def deal(raw, dealt, split):
+            nc.scalar.copy(
+                dealt.rearrange("p t m j -> p m j t")[:, :split],
+                raw.rearrange("p j (m t) -> p m j t", t=PACK)[:, :split],
+            )
+            if split < dealt.shape[2]:
                 nc.vector.tensor_copy(
                     dealt.rearrange("p (a t) m j -> p a m j t", a=2)[:, :, split:],
-                    w1_raw[g][c][:].rearrange("p j (m a t) -> p a m j t", a=2, t=2)[:, :, split:],
+                    raw.rearrange("p j (m a t) -> p a m j t", a=2, t=2)[:, :, split:],
+                )
+
+        def quantize_w1(g, dealt, cols):
+            for t in range(PACK):
+                nc.vector.quantize_mx(
+                    out=w1_codes[g][:, t, cols].bitcast(FP8X4),
+                    scales=w1_planes[g][:, t, cols],
+                    in_=dealt[:, t].rearrange("p m j -> p (m j)"),
                 )
 
         h_banks = [psum.tile([P, PACK, CHUNK], F32, name=f"h_bank{u}") for u in range(CHUNKS)]
@@ -132,44 +127,33 @@ def tile_picked_modgate_mlpsilu_p_kernel(tc, x_words, x_scales, gate, w1, w2_wor
                     stop=(g == PASSES - 1 and t == PACK - 1),
                 )
 
-        dealt0 = keep.tile([P, PACK, P, PACK], BF16, name="dealt0", tag="dealt0", align_bytes=64)
-        for c in range(HALVES):
-            deal(0, c, dealt0[:, :, c * HALF_M : (c + 1) * HALF_M, :])
-        nc.vector.quantize_mx(
-            out=w1_codes[0][:].rearrange("p t m -> p (t m)").bitcast(FP8X4),
-            scales=w1_planes[0][:].rearrange("p t m -> p (t m)"),
-            in_=dealt0[:].rearrange("p t m j -> p (t m j)"),
-        )
+        dealt0 = keep.tile([P, PACK, P, PACK], BF16, name="dealt0", align_bytes=64)
+        deal(w1_raw0[:], dealt0[:], SCALAR_M_PASS0)
+        quantize_w1(0, dealt0, slice(0, P))
         for u in range(CHUNKS):
             first_product(u, 0, picked0[u])
 
         for c in range(HALVES):
-            dealt = keep.tile([P, PACK, HALF_M, PACK], BF16, name=f"dealt1{c}", tag=f"dealt1{c}", align_bytes=64)
-            deal(1, c, dealt[:])
-            cols = slice(c * HALF_M, (c + 1) * HALF_M)
-            for t in range(PACK):
-                nc.vector.quantize_mx(
-                    out=w1_codes[1][:, t, cols].bitcast(FP8X4),
-                    scales=w1_planes[1][:, t, cols],
-                    in_=dealt[:, t].rearrange("p m j -> p (m j)"),
-                )
+            dealt1 = keep.tile([P, PACK, HALF_M, PACK], BF16, name=f"dealt1{c}", tag=f"dealt1{c}", align_bytes=64)
+            deal(w1_raw1[c][:], dealt1[:], SCALAR_M_PASS1[c])
+            quantize_w1(1, dealt1, slice(c * HALF_M, (c + 1) * HALF_M))
 
         def pick_scores(first, last, tag):
             scores = keep.tile([P, (last - first) * CHUNK], F32, name=f"scores{first}", tag=tag, align_bytes=64)
             nc.vector.tensor_copy(scores[:], gate_table[:].indirect(entries(first, last)))
             return scores
 
-        def hidden(u, words, tag):
-            first_product(u, 1, words)
-            h = keep.tile([P, CHUNK, PACK], BF16, name=f"h{u}", tag=tag, align_bytes=64)
-            nc.scalar.activation(h[:], h_banks[u][:].rearrange("p t n -> p n t"), SILU)
-            return h
+        def hidden(u):
+            first_product(u, 1, picked1[u])
+            h_u = keep.tile([P, CHUNK, PACK], BF16, name=f"h{u}", tag=f"h{u}", align_bytes=64)
+            nc.scalar.activation(h_u[:], h_banks[u][:].rearrange("p t n -> p n t"), SILU)
+            return h_u
 
-        def second_product(u, h):
+        def second_product(u):
             h_codes = keep.tile([P, CHUNK], U32, name=f"h_codes{u}", align_bytes=64)
             h_plane = keep.tile([P, CHUNK], U8, name=f"h_plane{u}", align_bytes=64)
             nc.vector.quantize_mx(
-                out=h_codes[:].bitcast(FP8X4), scales=h_plane[:], in_=h[:].rearrange("p n t -> p (n t)")
+                out=h_codes[:].bitcast(FP8X4), scales=h_plane[:], in_=h[u][:].rearrange("p n t -> p (n t)")
             )
             y_bank = psum.tile([P, CHUNK], F32, name=f"y_bank{u}")
             nc.tensor.matmul_mx(
@@ -185,24 +169,21 @@ def tile_picked_modgate_mlpsilu_p_kernel(tc, x_words, x_scales, gate, w1, w2_wor
 
         y = keep.tile([P, S], F32, name="y", align_bytes=64)
 
-        def fetch(u, y_bank):
-            nc.scalar.copy(y[:, u * CHUNK : (u + 1) * CHUNK], y_bank[:])
-
         def put_back(first, last, scores):
+            for u in range(first, last):
+                nc.scalar.copy(y[:, u * CHUNK : (u + 1) * CHUNK], y_banks[u][:])
             nc.vector.tensor_tensor(
-                window[:].indirect(entries(first, last)), y[:, first * CHUNK : last * CHUNK], scores, MULT
+                window[:].indirect(entries(first, last)), y[:, first * CHUNK : last * CHUNK], scores[:], MULT
             )
 
-        picked1 = pick_words(1, 0, 1, "picked10") + pick_words(1, 1, 2, "dealt11") + pick_words(1, 2, 4, "dealt10")
-        h = [hidden(u, picked1[u], f"h{u}") for u in range(CHUNKS)]
+        picked1 = pick_words(1, 0, 1, "picked10") + pick_words(1, 1, 2, "dealt11") + pick_words(1, 2, CHUNKS, "dealt10")
+        h = [hidden(u) for u in range(CHUNKS)]
         scores_first = pick_scores(0, 1, "scores0")
-        y_banks = [second_product(0, h[0])]
+        y_banks = [second_product(0)]
         scores_rest = pick_scores(1, CHUNKS, "h0")
-        y_banks.extend(second_product(u, h[u]) for u in range(1, CHUNKS))
-        fetch(0, y_banks[0])
-        put_back(0, 1, scores_first[:])
-        for u in range(1, CHUNKS):
-            fetch(u, y_banks[u])
-        put_back(1, CHUNKS, scores_rest[:])
+        y_banks.extend(second_product(u) for u in range(1, CHUNKS))
+
+        put_back(0, 1, scores_first)
+        put_back(1, CHUNKS, scores_rest)
 
         nc.sync.dma_start(out, window[:])

@@ -1,6 +1,7 @@
 from contextlib import ExitStack
 
 import concourse.mybir as mybir
+from concourse.masks import make_identity
 
 K, T, S, H, N = 1024, 1024, 512, 512, 128
 FLOPS = 2 * S * H * (K + N)
@@ -43,8 +44,8 @@ def tile_picked_modgate_mlpsilu_p_kernel(tc, x_words, x_scales, gate, w1, w2_wor
         nc.scalar.activation(warm_out[:], warm_in[:], SILU)
 
         x_table = [keep.tile([P, T], I32, name=f"x_table{g}", align_bytes=64) for g in range(PASSES)]
-        w1_raw0 = keep.tile([P, PACK, H], F32, name="w1_raw0", align_bytes=64)
-        w1_raw1 = [keep.tile([P, PACK, H // HALVES], F32, name=f"w1_raw1{c}", align_bytes=64) for c in range(HALVES)]
+        w1_raw0 = keep.tile([P, PACK, H], F32, name="w1_raw0", tag="raw0", align_bytes=64)
+        w1_raw1 = [keep.tile([P, PACK, H // HALVES], F32, name=f"w1_raw1{c}", tag=f"raw1{c}", align_bytes=64) for c in range(HALVES)]
         offsets = keep.tile([P, S // 16], U16, name="offsets")
 
         def load_x(g):
@@ -54,6 +55,8 @@ def tile_picked_modgate_mlpsilu_p_kernel(tc, x_words, x_scales, gate, w1, w2_wor
 
         load_x(0)
         nc.sync.dma_start(offsets[:], offs)
+        gate_row = keep.tile([P, T // P], F32, name="gate_row", tag="dealt0", align_bytes=64)
+        nc.sync.dma_start(gate_row[:], gate[0].rearrange("(p c) -> p c", p=P))
         for q in range(QUADRANTS):
             nc.sync.dma_start(
                 x_planes[32 * q : 32 * q + 4 * PASSES, :].bitcast(I32),
@@ -63,8 +66,6 @@ def tile_picked_modgate_mlpsilu_p_kernel(tc, x_words, x_scales, gate, w1, w2_wor
         for c in range(HALVES):
             nc.sync.dma_start(w1_raw1[c][:], w1_rows[1][:, :, c * (H // HALVES) : (c + 1) * (H // HALVES)])
         load_x(1)
-        gate_table = keep.tile([P, T], F32, name="gate_table", align_bytes=64)
-        nc.sync.dma_start(gate_table[:], gate)
         w2_codes = keep.tile([P, N], I32, name="w2_codes", align_bytes=64)
         nc.sync.dma_start(w2_codes[:], w2_words[0].rearrange("p n t -> p (n t)").bitcast(I32))
         w2_plane = keep.tile([P, N], U8, name="w2_plane", align_bytes=64)
@@ -77,6 +78,19 @@ def tile_picked_modgate_mlpsilu_p_kernel(tc, x_words, x_scales, gate, w1, w2_wor
 
         window = keep.tile([P, T], F32, name="window", align_bytes=64)
         nc.vector.memset(window[:], 0.0)
+
+        identity = keep.tile([P, P], F32, name="identity", align_bytes=64)
+        make_identity(nc, identity[:])
+        gate_table = keep.tile([P, T], F32, name="gate_table", align_bytes=64)
+        for a in range(2):
+            spread = psum.tile([P, PACK, P], F32, name=f"spread{a}", tag=f"y_bank{a}")
+            for c in range(PACK):
+                column = gate_row[:, a * PACK + c : a * PACK + c + 1]
+                nc.tensor.transpose(spread[:, c, :], column.to_broadcast([P, P]), identity[:])
+            nc.scalar.copy(
+                gate_table[:].rearrange("p (n a c) -> p a n c", a=2, c=PACK)[:, a],
+                spread[:].rearrange("p c n -> p n c"),
+            )
 
         def entries(first, last):
             return offsets[:, first * LIST_COLS : last * LIST_COLS]
@@ -127,9 +141,16 @@ def tile_picked_modgate_mlpsilu_p_kernel(tc, x_words, x_scales, gate, w1, w2_wor
                     stop=(g == PASSES - 1 and t == PACK - 1),
                 )
 
-        dealt0 = keep.tile([P, PACK, P, PACK], BF16, name="dealt0", align_bytes=64)
+        def pick_scores(first, last, tag):
+            scores = keep.tile([P, (last - first) * CHUNK], F32, name=f"scores{first}", tag=tag, align_bytes=64)
+            nc.vector.tensor_copy(scores[:], gate_table[:].indirect(entries(first, last)))
+            return scores
+
+        dealt0 = keep.tile([P, PACK, P, PACK], BF16, name="dealt0", tag="dealt0", align_bytes=64)
         deal(w1_raw0[:], dealt0[:], SCALAR_M_PASS0)
+        scores_first = pick_scores(0, 1, "scores0")
         quantize_w1(0, dealt0, slice(0, P))
+        scores_last = pick_scores(1, 2, "raw0")
         for u in range(CHUNKS):
             first_product(u, 0, picked0[u])
 
@@ -138,52 +159,69 @@ def tile_picked_modgate_mlpsilu_p_kernel(tc, x_words, x_scales, gate, w1, w2_wor
             deal(w1_raw1[c][:], dealt1[:], SCALAR_M_PASS1[c])
             quantize_w1(1, dealt1, slice(c * HALF_M, (c + 1) * HALF_M))
 
-        def pick_scores(first, last, tag):
-            scores = keep.tile([P, (last - first) * CHUNK], F32, name=f"scores{first}", tag=tag, align_bytes=64)
-            nc.vector.tensor_copy(scores[:], gate_table[:].indirect(entries(first, last)))
-            return scores
-
-        def hidden(u):
-            first_product(u, 1, picked1[u])
-            h_u = keep.tile([P, CHUNK, PACK], BF16, name=f"h{u}", tag=f"h{u}", align_bytes=64)
-            nc.scalar.activation(h_u[:], h_banks[u][:].rearrange("p t n -> p n t"), SILU)
+        def hidden(u, tag, pieces=1):
+            h_u = keep.tile([P, CHUNK * PACK], BF16, name=f"h{u}", tag=tag, align_bytes=64)
+            width = CHUNK // pieces
+            for v in range(pieces):
+                nc.scalar.activation(
+                    h_u[:, v * width * PACK : (v + 1) * width * PACK].rearrange("p (n t) -> p n t", t=PACK),
+                    h_banks[u][:, :, v * width : (v + 1) * width].rearrange("p t n -> p n t"),
+                    SILU,
+                )
             return h_u
 
-        def second_product(u):
-            h_codes = keep.tile([P, CHUNK], U32, name=f"h_codes{u}", align_bytes=64)
-            h_plane = keep.tile([P, CHUNK], U8, name=f"h_plane{u}", align_bytes=64)
-            nc.vector.quantize_mx(
-                out=h_codes[:].bitcast(FP8X4), scales=h_plane[:], in_=h[u][:].rearrange("p n t -> p (n t)")
-            )
-            y_bank = psum.tile([P, CHUNK], F32, name=f"y_bank{u}")
-            nc.tensor.matmul_mx(
-                out=y_bank[:],
-                lhsT=w2_codes[:].bitcast(FP8X4),
-                lhsT_scale=w2_plane[:],
-                rhs=h_codes[:].bitcast(FP8X4),
-                rhs_scale=h_plane[:],
-                start=True,
-                stop=True,
-            )
+        def second_product(u, h_u, pieces=1):
+            h_codes = keep.tile([P, CHUNK], U32, name=f"h_codes{u}", tag=f"h_codes{u}", align_bytes=64)
+            h_plane = keep.tile([P, CHUNK], U8, name=f"h_plane{u}", tag=f"h_plane{u}", align_bytes=64)
+            y_bank = psum.tile([P, CHUNK], F32, name=f"y_bank{u}", tag=f"y_bank{u}")
+            width = CHUNK // pieces
+            for v in range(pieces):
+                cols = slice(v * width, (v + 1) * width)
+                nc.vector.quantize_mx(
+                    out=h_codes[:, cols].bitcast(FP8X4),
+                    scales=h_plane[:, cols],
+                    in_=h_u[:, v * width * PACK : (v + 1) * width * PACK],
+                )
+                nc.tensor.matmul_mx(
+                    out=y_bank[:, cols],
+                    lhsT=w2_codes[:].bitcast(FP8X4),
+                    lhsT_scale=w2_plane[:],
+                    rhs=h_codes[:, cols].bitcast(FP8X4),
+                    rhs_scale=h_plane[:, cols],
+                    start=True,
+                    stop=True,
+                )
             return y_bank
 
         y = keep.tile([P, S], F32, name="y", align_bytes=64)
 
+        def fetch(u, y_bank):
+            nc.scalar.copy(y[:, u * CHUNK : (u + 1) * CHUNK], y_bank[:])
+
         def put_back(first, last, scores):
-            for u in range(first, last):
-                nc.scalar.copy(y[:, u * CHUNK : (u + 1) * CHUNK], y_banks[u][:])
             nc.vector.tensor_tensor(
-                window[:].indirect(entries(first, last)), y[:, first * CHUNK : last * CHUNK], scores[:], MULT
+                window[:].indirect(entries(first, last)), y[:, first * CHUNK : last * CHUNK], scores, MULT
             )
 
-        picked1 = pick_words(1, 0, 1, "picked10") + pick_words(1, 1, 2, "dealt11") + pick_words(1, 2, CHUNKS, "dealt10")
-        h = [hidden(u) for u in range(CHUNKS)]
-        scores_first = pick_scores(0, 1, "scores0")
-        y_banks = [second_product(0)]
-        scores_rest = pick_scores(1, CHUNKS, "h0")
-        y_banks.extend(second_product(u) for u in range(1, CHUNKS))
-
-        put_back(0, 1, scores_first)
-        put_back(1, CHUNKS, scores_rest)
-
+        picked1 = pick_words(1, 0, 1, "raw11")
+        later = keep.tile([P, S - CHUNK], U32, name="later", tag="dealt11", align_bytes=64)
+        for first, last in ((1, 2), (2, CHUNKS)):
+            nc.vector.tensor_copy(
+                later[:, (first - 1) * CHUNK : (last - 1) * CHUNK],
+                x_table[1][:].bitcast(U32).indirect(entries(first, last)),
+            )
+        picked1.extend(later[:, v * CHUNK : (v + 1) * CHUNK] for v in range(CHUNKS - 1))
+        for u in range(CHUNKS):
+            first_product(u, 1, picked1[u])
+        scores_rest = pick_scores(2, CHUNKS, "raw11")
+        h = [hidden(0, "h0", 2), hidden(1, "h1")]
+        y_banks = [second_product(0, h[0], 2), second_product(1, h[1])]
+        fetch(0, y_banks[0])
+        put_back(0, 1, scores_first[:])
+        h.extend((hidden(2, "h_codes0"), hidden(3, "h_plane0")))
+        y_banks.extend(second_product(u, h[u]) for u in (2, 3))
+        for u in range(1, CHUNKS):
+            fetch(u, y_banks[u])
+        put_back(1, 2, scores_last[:])
+        put_back(2, CHUNKS, scores_rest[:])
         nc.sync.dma_start(out, window[:])

@@ -14,25 +14,27 @@ U16 = mybir.dt.uint16
 U8 = mybir.dt.uint8
 FP8X4 = mybir.dt.float8_e4m3fn_x4
 SILU = mybir.ActivationFunctionType.Silu
+COPY = mybir.ActivationFunctionType.Copy
 MULT = mybir.AluOpType.mult
+ADD = mybir.AluOpType.add
 
 P = 128
 PACK = 4
 PASSES = K // (P * PACK)
 QUADRANTS = 4
-HALVES = 2
-HALF_M = P // HALVES
 CHUNK = 128
 CHUNKS = S // CHUNK
+STORES = 4
+SCALAR_M_PASS1 = 32
 LIST_COLS = CHUNK // 16
 SCALAR_M_PASS0 = 40
-SCALAR_M_PASS1 = (HALF_M, 24)
 
 
 def tile_picked_modgate_mlpsilu_p_kernel(tc, x_words, x_scales, gate, w1, w2_words, w2_scales, offs, out):
     nc = tc.nc
     with ExitStack() as ctx:
         keep = ctx.enter_context(tc.tile_pool(name="keep", bufs=1))
+        late = ctx.enter_context(tc.tile_pool(name="late", bufs=1))
         psum = ctx.enter_context(tc.psum_pool(name="psum", bufs=1))
 
         x_planes = keep.tile([P, T], U8, name="x_planes", align_bytes=64)
@@ -44,8 +46,8 @@ def tile_picked_modgate_mlpsilu_p_kernel(tc, x_words, x_scales, gate, w1, w2_wor
         nc.scalar.activation(warm_out[:], warm_in[:], SILU)
 
         x_table = [keep.tile([P, T], I32, name=f"x_table{g}", align_bytes=64) for g in range(PASSES)]
-        w1_raw0 = keep.tile([P, PACK, H], F32, name="w1_raw0", tag="raw0", align_bytes=64)
-        w1_raw1 = [keep.tile([P, PACK, H // HALVES], F32, name=f"w1_raw1{c}", tag=f"raw1{c}", align_bytes=64) for c in range(HALVES)]
+        w1_raw0 = late.tile([P, PACK, H], F32, name="w1_raw0", align_bytes=64, offset=8192)
+        w1_raw1 = late.tile([P, PACK, H], F32, name="w1_raw1", align_bytes=64, offset=16384)
         offsets = keep.tile([P, S // 16], U16, name="offsets")
 
         def load_x(g):
@@ -63,8 +65,7 @@ def tile_picked_modgate_mlpsilu_p_kernel(tc, x_words, x_scales, gate, w1, w2_wor
                 x_scales[:, 4 * q : 4 * q + 4, :].bitcast(I32),
             )
         nc.sync.dma_start(w1_raw0[:], w1_rows[0])
-        for c in range(HALVES):
-            nc.sync.dma_start(w1_raw1[c][:], w1_rows[1][:, :, c * (H // HALVES) : (c + 1) * (H // HALVES)])
+        nc.sync.dma_start(w1_raw1[:], w1_rows[1])
         load_x(1)
         w2_codes = keep.tile([P, N], I32, name="w2_codes", align_bytes=64)
         nc.sync.dma_start(w2_codes[:], w2_words[0].rearrange("p n t -> p (n t)").bitcast(I32))
@@ -76,8 +77,9 @@ def tile_picked_modgate_mlpsilu_p_kernel(tc, x_words, x_scales, gate, w1, w2_wor
                 w2_scales[0, 4 * q : 4 * q + 4, :].bitcast(I32),
             )
 
-        window = keep.tile([P, T], F32, name="window", align_bytes=64)
-        nc.vector.memset(window[:], 0.0)
+        windows = [keep.tile([P, T], F32, name=f"window{e}", align_bytes=64) for e in range(2)]
+        for window in windows:
+            nc.vector.memset(window[:], 0.0)
 
         identity = keep.tile([P, P], F32, name="identity", align_bytes=64)
         make_identity(nc, identity[:])
@@ -118,11 +120,11 @@ def tile_picked_modgate_mlpsilu_p_kernel(tc, x_words, x_scales, gate, w1, w2_wor
                     raw.rearrange("p j (m a t) -> p a m j t", a=2, t=2)[:, :, split:],
                 )
 
-        def quantize_w1(g, dealt, cols):
-            for t in range(PACK):
+        def quantize_w1(g, dealt, first):
+            for t in range(dealt.shape[1]):
                 nc.vector.quantize_mx(
-                    out=w1_codes[g][:, t, cols].bitcast(FP8X4),
-                    scales=w1_planes[g][:, t, cols],
+                    out=w1_codes[g][:, first + t, :].bitcast(FP8X4),
+                    scales=w1_planes[g][:, first + t, :],
                     in_=dealt[:, t].rearrange("p m j -> p (m j)"),
                 )
 
@@ -141,23 +143,29 @@ def tile_picked_modgate_mlpsilu_p_kernel(tc, x_words, x_scales, gate, w1, w2_wor
                     stop=(g == PASSES - 1 and t == PACK - 1),
                 )
 
-        def pick_scores(first, last, tag):
-            scores = keep.tile([P, (last - first) * CHUNK], F32, name=f"scores{first}", tag=tag, align_bytes=64)
-            nc.vector.tensor_copy(scores[:], gate_table[:].indirect(entries(first, last)))
-            return scores
-
         dealt0 = keep.tile([P, PACK, P, PACK], BF16, name="dealt0", tag="dealt0", align_bytes=64)
         deal(w1_raw0[:], dealt0[:], SCALAR_M_PASS0)
-        scores_first = pick_scores(0, 1, "scores0")
-        quantize_w1(0, dealt0, slice(0, P))
-        scores_last = pick_scores(1, 2, "raw0")
+        quantize_w1(0, dealt0[:], 0)
         for u in range(CHUNKS):
             first_product(u, 0, picked0[u])
 
-        for c in range(HALVES):
-            dealt1 = keep.tile([P, PACK, HALF_M, PACK], BF16, name=f"dealt1{c}", tag=f"dealt1{c}", align_bytes=64)
-            deal(w1_raw1[c][:], dealt1[:], SCALAR_M_PASS1[c])
-            quantize_w1(1, dealt1, slice(c * HALF_M, (c + 1) * HALF_M))
+        def pick_scores(first, last, offset):
+            picked = late.tile(
+                [P, (last - first) * CHUNK], F32, name=f"scores{first}", align_bytes=64, offset=offset
+            )
+            nc.scalar.activation(picked[:], gate_table[:].indirect(entries(first, last)), COPY)
+            return [picked[:, v * CHUNK : (v + 1) * CHUNK] for v in range(last - first)]
+
+        scores = pick_scores(0, 1, 2048) + pick_scores(1, 2, 2560)
+
+        pairs = [keep.tile([P, 2, P, PACK], BF16, name=f"dealt1{a}", tag=f"dealt1{a}", align_bytes=64) for a in range(2)]
+        raw_pairs = w1_raw1[:].rearrange("p j (m a t) -> p a m j t", a=2, t=2)
+        first_pair = pairs[0][:].rearrange("p t m j -> p m j t")
+        nc.vector.tensor_copy(first_pair[:, SCALAR_M_PASS1:], raw_pairs[:, 0, SCALAR_M_PASS1:])
+        nc.scalar.copy(first_pair[:, :SCALAR_M_PASS1], raw_pairs[:, 0, :SCALAR_M_PASS1])
+        nc.scalar.copy(pairs[1][:].rearrange("p t m j -> p m j t"), raw_pairs[:, 1])
+        quantize_w1(1, pairs[0][:], 0)
+        scores.extend(pick_scores(2, CHUNKS, 16384))
 
         def hidden(u, tag, pieces=1):
             h_u = keep.tile([P, CHUNK * PACK], BF16, name=f"h{u}", tag=tag, align_bytes=64)
@@ -170,8 +178,8 @@ def tile_picked_modgate_mlpsilu_p_kernel(tc, x_words, x_scales, gate, w1, w2_wor
                 )
             return h_u
 
-        def second_product(u, h_u, pieces=1):
-            h_codes = keep.tile([P, CHUNK], U32, name=f"h_codes{u}", tag=f"h_codes{u}", align_bytes=64)
+        def second_product(u, h_u, offset, pieces=1):
+            h_codes = late.tile([P, CHUNK], U32, name=f"h_codes{u}", align_bytes=64, offset=offset)
             h_plane = keep.tile([P, CHUNK], U8, name=f"h_plane{u}", tag=f"h_plane{u}", align_bytes=64)
             y_bank = psum.tile([P, CHUNK], F32, name=f"y_bank{u}", tag=f"y_bank{u}")
             width = CHUNK // pieces
@@ -193,35 +201,49 @@ def tile_picked_modgate_mlpsilu_p_kernel(tc, x_words, x_scales, gate, w1, w2_wor
                 )
             return y_bank
 
-        y = keep.tile([P, S], F32, name="y", align_bytes=64)
+        weighted = keep.tile([P, S], F32, name="weighted", align_bytes=64)
 
-        def fetch(u, y_bank):
-            nc.scalar.copy(y[:, u * CHUNK : (u + 1) * CHUNK], y_bank[:])
-
-        def put_back(first, last, scores):
+        def weigh(u, y_bank, first=0, last=CHUNK):
             nc.vector.tensor_tensor(
-                window[:].indirect(entries(first, last)), y[:, first * CHUNK : last * CHUNK], scores, MULT
+                weighted[:, u * CHUNK + first : u * CHUNK + last], y_bank[:, first:last], scores[u][:, first:last], MULT
             )
 
-        picked1 = pick_words(1, 0, 1, "raw11")
-        later = keep.tile([P, S - CHUNK], U32, name="later", tag="dealt11", align_bytes=64)
+        def put_back_vector(first, last):
+            nc.vector.tensor_copy(windows[0][:].indirect(offsets[:, first // 16 : last // 16]), weighted[:, first:last])
+
+        def put_back_scalar(first, last):
+            nc.scalar.activation(
+                windows[1][:].indirect(offsets[:, first // 16 : last // 16]), weighted[:, first:last], COPY
+            )
+
+        first_words = late.tile([P, CHUNK], U32, name="first_words", align_bytes=64, offset=0)
+        nc.vector.tensor_copy(first_words[:], x_table[1][:].bitcast(U32).indirect(entries(0, 1)))
+        picked1 = [first_words[:]]
+        quantize_w1(1, pairs[1][:], 2)
+        later = keep.tile([P, S - CHUNK], U32, name="later", align_bytes=64)
         for first, last in ((1, 2), (2, CHUNKS)):
             nc.vector.tensor_copy(
                 later[:, (first - 1) * CHUNK : (last - 1) * CHUNK],
                 x_table[1][:].bitcast(U32).indirect(entries(first, last)),
             )
         picked1.extend(later[:, v * CHUNK : (v + 1) * CHUNK] for v in range(CHUNKS - 1))
-        for u in range(CHUNKS):
+        for u in (0, 1, 3, 2):
             first_product(u, 1, picked1[u])
-        scores_rest = pick_scores(2, CHUNKS, "raw11")
-        h = [hidden(0, "h0", 2), hidden(1, "h1")]
-        y_banks = [second_product(0, h[0], 2), second_product(1, h[1])]
-        fetch(0, y_banks[0])
-        put_back(0, 1, scores_first[:])
-        h.extend((hidden(2, "h_codes0"), hidden(3, "h_plane0")))
-        y_banks.extend(second_product(u, h[u]) for u in (2, 3))
-        for u in range(1, CHUNKS):
-            fetch(u, y_banks[u])
-        put_back(1, 2, scores_last[:])
-        put_back(2, CHUNKS, scores_rest[:])
-        nc.sync.dma_start(out, window[:])
+        h = {0: hidden(0, "h0", 2), 1: hidden(1, "h1"), 3: hidden(3, "h3"), 2: hidden(2, "h2")}
+        y0 = second_product(0, h[0], 4096, 2)
+        y1 = second_product(1, h[1], 4608)
+        weigh(0, y0)
+        y3 = second_product(3, h[3], 2048)
+        weigh(1, y1)
+        y2 = second_product(2, h[2], 2560)
+        put_back_scalar(0, 160)
+        weigh(3, y3)
+        weigh(2, y2, 0, 96)
+        weigh(2, y2, 96, CHUNK)
+        put_back_vector(160, 352)
+        put_back_scalar(352, S)
+        merged = keep.tile([P, T], F32, name="merged", align_bytes=64)
+        for c in range(STORES):
+            cols = slice(c * (T // STORES), (c + 1) * (T // STORES))
+            nc.vector.tensor_tensor(merged[:, cols], windows[0][:, cols], windows[1][:, cols], ADD)
+            nc.sync.dma_start(out[:, cols], merged[:, cols])

@@ -16,7 +16,6 @@ FP8X4 = mybir.dt.float8_e4m3fn_x4
 SILU = mybir.ActivationFunctionType.Silu
 COPY = mybir.ActivationFunctionType.Copy
 MULT = mybir.AluOpType.mult
-ADD = mybir.AluOpType.add
 
 P = 128
 PACK = 4
@@ -24,17 +23,17 @@ PASSES = K // (P * PACK)
 QUADRANTS = 4
 CHUNK = 128
 CHUNKS = S // CHUNK
-STORES = 4
-SCALAR_M_PASS1 = 32
 LIST_COLS = CHUNK // 16
+FIRST_PIECES = 2
+PAIR = 2
 SCALAR_M_PASS0 = 40
+SCALAR_M_PASS1 = 32
 
 
 def tile_picked_modgate_mlpsilu_p_kernel(tc, x_words, x_scales, gate, w1, w2_words, w2_scales, offs, out):
     nc = tc.nc
     with ExitStack() as ctx:
         keep = ctx.enter_context(tc.tile_pool(name="keep", bufs=1))
-        late = ctx.enter_context(tc.tile_pool(name="late", bufs=1))
         psum = ctx.enter_context(tc.psum_pool(name="psum", bufs=1))
 
         x_planes = keep.tile([P, T], U8, name="x_planes", align_bytes=64)
@@ -46,8 +45,7 @@ def tile_picked_modgate_mlpsilu_p_kernel(tc, x_words, x_scales, gate, w1, w2_wor
         nc.scalar.activation(warm_out[:], warm_in[:], SILU)
 
         x_table = [keep.tile([P, T], I32, name=f"x_table{g}", align_bytes=64) for g in range(PASSES)]
-        w1_raw0 = late.tile([P, PACK, H], F32, name="w1_raw0", align_bytes=64, offset=8192)
-        w1_raw1 = late.tile([P, PACK, H], F32, name="w1_raw1", align_bytes=64, offset=16384)
+        w1_raw = [keep.tile([P, PACK, H], F32, name=f"w1_raw{g}", align_bytes=64) for g in range(PASSES)]
         offsets = keep.tile([P, S // 16], U16, name="offsets")
 
         def load_x(g):
@@ -64,8 +62,8 @@ def tile_picked_modgate_mlpsilu_p_kernel(tc, x_words, x_scales, gate, w1, w2_wor
                 x_planes[32 * q : 32 * q + 4 * PASSES, :].bitcast(I32),
                 x_scales[:, 4 * q : 4 * q + 4, :].bitcast(I32),
             )
-        nc.sync.dma_start(w1_raw0[:], w1_rows[0])
-        nc.sync.dma_start(w1_raw1[:], w1_rows[1])
+        for g in range(PASSES):
+            nc.sync.dma_start(w1_raw[g][:], w1_rows[g])
         load_x(1)
         w2_codes = keep.tile([P, N], I32, name="w2_codes", align_bytes=64)
         nc.sync.dma_start(w2_codes[:], w2_words[0].rearrange("p n t -> p (n t)").bitcast(I32))
@@ -77,48 +75,38 @@ def tile_picked_modgate_mlpsilu_p_kernel(tc, x_words, x_scales, gate, w1, w2_wor
                 w2_scales[0, 4 * q : 4 * q + 4, :].bitcast(I32),
             )
 
-        windows = [keep.tile([P, T], F32, name=f"window{e}", align_bytes=64) for e in range(2)]
-        for window in windows:
-            nc.vector.memset(window[:], 0.0)
+        window = keep.tile([P, T], F32, name="window", align_bytes=64)
+        nc.vector.memset(window[:], 0.0)
 
         identity = keep.tile([P, P], F32, name="identity", align_bytes=64)
         make_identity(nc, identity[:])
         gate_table = keep.tile([P, T], F32, name="gate_table", align_bytes=64)
-        for a in range(2):
+        for a in range(T // P // PACK):
             spread = psum.tile([P, PACK, P], F32, name=f"spread{a}", tag=f"y_bank{a}")
             for c in range(PACK):
                 column = gate_row[:, a * PACK + c : a * PACK + c + 1]
                 nc.tensor.transpose(spread[:, c, :], column.to_broadcast([P, P]), identity[:])
             nc.scalar.copy(
-                gate_table[:].rearrange("p (n a c) -> p a n c", a=2, c=PACK)[:, a],
+                gate_table[:].rearrange("p (n a c) -> p a n c", n=P, c=PACK)[:, a],
                 spread[:].rearrange("p c n -> p n c"),
             )
 
         def entries(first, last):
             return offsets[:, first * LIST_COLS : last * LIST_COLS]
 
-        def pick_words(g, first, last, tag):
-            words = keep.tile([P, (last - first) * CHUNK], U32, name=f"picked{g}{first}", tag=tag, align_bytes=64)
-            nc.vector.tensor_copy(words[:], x_table[g][:].bitcast(U32).indirect(entries(first, last)))
-            return [words[:, v * CHUNK : (v + 1) * CHUNK] for v in range(last - first)]
+        picked = [keep.tile([P, S], U32, name=f"picked{g}", align_bytes=64) for g in range(PASSES)]
 
-        picked0 = pick_words(0, 0, CHUNKS, "picked0")
+        def pick_words(g, first, last):
+            nc.vector.tensor_copy(
+                picked[g][:, first * CHUNK : last * CHUNK], x_table[g][:].bitcast(U32).indirect(entries(first, last))
+            )
+
+        pick_words(0, 0, CHUNKS)
         picked_planes = keep.tile([P, S], U8, name="picked_planes", align_bytes=64)
         nc.vector.tensor_copy(picked_planes[:], x_planes[:].indirect(offsets[:]))
 
         w1_codes = [keep.tile([P, PACK, P], U32, name=f"w1_codes{g}", align_bytes=64) for g in range(PASSES)]
         w1_planes = [keep.tile([P, PACK, P], U8, name=f"w1_planes{g}", align_bytes=64) for g in range(PASSES)]
-
-        def deal(raw, dealt, split):
-            nc.scalar.copy(
-                dealt.rearrange("p t m j -> p m j t")[:, :split],
-                raw.rearrange("p j (m t) -> p m j t", t=PACK)[:, :split],
-            )
-            if split < dealt.shape[2]:
-                nc.vector.tensor_copy(
-                    dealt.rearrange("p (a t) m j -> p a m j t", a=2)[:, :, split:],
-                    raw.rearrange("p j (m a t) -> p a m j t", a=2, t=2)[:, :, split:],
-                )
 
         def quantize_w1(g, dealt, first):
             for t in range(dealt.shape[1]):
@@ -130,42 +118,52 @@ def tile_picked_modgate_mlpsilu_p_kernel(tc, x_words, x_scales, gate, w1, w2_wor
 
         h_banks = [psum.tile([P, PACK, CHUNK], F32, name=f"h_bank{u}") for u in range(CHUNKS)]
 
-        def first_product(u, g, words):
+        def first_product(u, g):
             tokens = slice(u * CHUNK, (u + 1) * CHUNK)
             for t in range(PACK):
                 nc.tensor.matmul_mx(
                     out=h_banks[u][:, t, :],
                     lhsT=w1_codes[g][:, t, :].bitcast(FP8X4),
                     lhsT_scale=w1_planes[g][:, t, :],
-                    rhs=words.bitcast(FP8X4),
+                    rhs=picked[g][:, tokens].bitcast(FP8X4),
                     rhs_scale=picked_planes[4 * g :, tokens],
                     start=(g == 0 and t == 0),
                     stop=(g == PASSES - 1 and t == PACK - 1),
                 )
 
         dealt0 = keep.tile([P, PACK, P, PACK], BF16, name="dealt0", tag="dealt0", align_bytes=64)
-        deal(w1_raw0[:], dealt0[:], SCALAR_M_PASS0)
+        nc.scalar.copy(
+            dealt0[:].rearrange("p t m j -> p m j t")[:, :SCALAR_M_PASS0],
+            w1_raw[0][:].rearrange("p j (m t) -> p m j t", t=PACK)[:, :SCALAR_M_PASS0],
+        )
+        nc.vector.tensor_copy(
+            dealt0[:].rearrange("p (a t) m j -> p a m j t", t=PAIR)[:, :, SCALAR_M_PASS0:],
+            w1_raw[0][:].rearrange("p j (m a t) -> p a m j t", a=PACK // PAIR, t=PAIR)[:, :, SCALAR_M_PASS0:],
+        )
         quantize_w1(0, dealt0[:], 0)
         for u in range(CHUNKS):
-            first_product(u, 0, picked0[u])
+            first_product(u, 0)
 
-        def pick_scores(first, last, offset):
-            picked = late.tile(
-                [P, (last - first) * CHUNK], F32, name=f"scores{first}", align_bytes=64, offset=offset
-            )
-            nc.scalar.activation(picked[:], gate_table[:].indirect(entries(first, last)), COPY)
-            return [picked[:, v * CHUNK : (v + 1) * CHUNK] for v in range(last - first)]
+        def pick_scores(first, last, tag):
+            scores = keep.tile([P, (last - first) * CHUNK], F32, name=f"scores{first}", tag=tag, align_bytes=64)
+            nc.scalar.activation(scores[:], gate_table[:].indirect(entries(first, last)), COPY)
+            return scores
 
-        scores = pick_scores(0, 1, 2048) + pick_scores(1, 2, 2560)
+        scores_early = pick_scores(0, 2, "scores_early")
 
-        pairs = [keep.tile([P, 2, P, PACK], BF16, name=f"dealt1{a}", tag=f"dealt1{a}", align_bytes=64) for a in range(2)]
-        raw_pairs = w1_raw1[:].rearrange("p j (m a t) -> p a m j t", a=2, t=2)
-        first_pair = pairs[0][:].rearrange("p t m j -> p m j t")
+        dealt1 = [keep.tile([P, PAIR, P, PACK], BF16, name=f"dealt1{a}", align_bytes=64) for a in range(PACK // PAIR)]
+        raw_pairs = w1_raw[1][:].rearrange("p j (m a t) -> p a m j t", a=PACK // PAIR, t=PAIR)
+        first_pair = dealt1[0][:].rearrange("p t m j -> p m j t")
         nc.vector.tensor_copy(first_pair[:, SCALAR_M_PASS1:], raw_pairs[:, 0, SCALAR_M_PASS1:])
         nc.scalar.copy(first_pair[:, :SCALAR_M_PASS1], raw_pairs[:, 0, :SCALAR_M_PASS1])
-        nc.scalar.copy(pairs[1][:].rearrange("p t m j -> p m j t"), raw_pairs[:, 1])
-        quantize_w1(1, pairs[0][:], 0)
-        scores.extend(pick_scores(2, CHUNKS, 16384))
+        nc.scalar.copy(dealt1[1][:].rearrange("p t m j -> p m j t"), raw_pairs[:, 1])
+        quantize_w1(1, dealt1[0][:], 0)
+        pick_words(1, 0, 1)
+        quantize_w1(1, dealt1[1][:], PAIR)
+        for u in range(1, CHUNKS):
+            pick_words(1, u, u + 1)
+        for u in range(CHUNKS):
+            first_product(u, 1)
 
         def hidden(u, tag, pieces=1):
             h_u = keep.tile([P, CHUNK * PACK], BF16, name=f"h{u}", tag=tag, align_bytes=64)
@@ -178,8 +176,8 @@ def tile_picked_modgate_mlpsilu_p_kernel(tc, x_words, x_scales, gate, w1, w2_wor
                 )
             return h_u
 
-        def second_product(u, h_u, offset, pieces=1):
-            h_codes = late.tile([P, CHUNK], U32, name=f"h_codes{u}", align_bytes=64, offset=offset)
+        def second_product(u, h_u, pieces=1):
+            h_codes = keep.tile([P, CHUNK], U32, name=f"h_codes{u}", tag=f"h_codes{u}", align_bytes=64)
             h_plane = keep.tile([P, CHUNK], U8, name=f"h_plane{u}", tag=f"h_plane{u}", align_bytes=64)
             y_bank = psum.tile([P, CHUNK], F32, name=f"y_bank{u}", tag=f"y_bank{u}")
             width = CHUNK // pieces
@@ -201,49 +199,26 @@ def tile_picked_modgate_mlpsilu_p_kernel(tc, x_words, x_scales, gate, w1, w2_wor
                 )
             return y_bank
 
-        weighted = keep.tile([P, S], F32, name="weighted", align_bytes=64)
+        y = keep.tile([P, S], F32, name="y", align_bytes=64)
 
-        def weigh(u, y_bank, first=0, last=CHUNK):
+        def fetch(u, y_bank):
+            nc.scalar.copy(y[:, u * CHUNK : (u + 1) * CHUNK], y_bank[:])
+
+        def put_back(first, last, scores):
             nc.vector.tensor_tensor(
-                weighted[:, u * CHUNK + first : u * CHUNK + last], y_bank[:, first:last], scores[u][:, first:last], MULT
+                window[:].indirect(entries(first, last)), y[:, first * CHUNK : last * CHUNK], scores, MULT
             )
 
-        def put_back_vector(first, last):
-            nc.vector.tensor_copy(windows[0][:].indirect(offsets[:, first // 16 : last // 16]), weighted[:, first:last])
-
-        def put_back_scalar(first, last):
-            nc.scalar.activation(
-                windows[1][:].indirect(offsets[:, first // 16 : last // 16]), weighted[:, first:last], COPY
-            )
-
-        first_words = late.tile([P, CHUNK], U32, name="first_words", align_bytes=64, offset=0)
-        nc.vector.tensor_copy(first_words[:], x_table[1][:].bitcast(U32).indirect(entries(0, 1)))
-        picked1 = [first_words[:]]
-        quantize_w1(1, pairs[1][:], 2)
-        later = keep.tile([P, S - CHUNK], U32, name="later", align_bytes=64)
-        for first, last in ((1, 2), (2, CHUNKS)):
-            nc.vector.tensor_copy(
-                later[:, (first - 1) * CHUNK : (last - 1) * CHUNK],
-                x_table[1][:].bitcast(U32).indirect(entries(first, last)),
-            )
-        picked1.extend(later[:, v * CHUNK : (v + 1) * CHUNK] for v in range(CHUNKS - 1))
-        for u in (0, 1, 3, 2):
-            first_product(u, 1, picked1[u])
-        h = {0: hidden(0, "h0", 2), 1: hidden(1, "h1"), 3: hidden(3, "h3"), 2: hidden(2, "h2")}
-        y0 = second_product(0, h[0], 4096, 2)
-        y1 = second_product(1, h[1], 4608)
-        weigh(0, y0)
-        y3 = second_product(3, h[3], 2048)
-        weigh(1, y1)
-        y2 = second_product(2, h[2], 2560)
-        put_back_scalar(0, 160)
-        weigh(3, y3)
-        weigh(2, y2, 0, 96)
-        weigh(2, y2, 96, CHUNK)
-        put_back_vector(160, 352)
-        put_back_scalar(352, S)
-        merged = keep.tile([P, T], F32, name="merged", align_bytes=64)
-        for c in range(STORES):
-            cols = slice(c * (T // STORES), (c + 1) * (T // STORES))
-            nc.vector.tensor_tensor(merged[:, cols], windows[0][:, cols], windows[1][:, cols], ADD)
-            nc.sync.dma_start(out[:, cols], merged[:, cols])
+        h = [hidden(0, "h0", FIRST_PIECES), hidden(1, "h1")]
+        y_banks = [second_product(0, h[0], FIRST_PIECES), second_product(1, h[1])]
+        fetch(0, y_banks[0])
+        put_back(0, 1, scores_early[:, :CHUNK])
+        h.extend((hidden(2, "h_codes0"), hidden(3, "h_plane0")))
+        y_banks.extend(second_product(u, h[u]) for u in (2, 3))
+        fetch(1, y_banks[1])
+        scores_late = pick_scores(2, CHUNKS, "h_codes0")
+        for u in range(2, CHUNKS):
+            fetch(u, y_banks[u])
+        put_back(1, 2, scores_early[:, CHUNK:])
+        put_back(2, CHUNKS, scores_late[:])
+        nc.sync.dma_start(out, window[:])

@@ -153,10 +153,10 @@ def tile_picked_modgate_mlpsilu_p_kernel(tc, x_words, x_scales, gate, w1, w2_wor
 
         dealt1 = [keep.tile([P, PAIR, P, PACK], BF16, name=f"dealt1{a}", align_bytes=64) for a in range(PACK // PAIR)]
         raw_pairs = w1_raw[1][:].rearrange("p j (m a t) -> p a m j t", a=PACK // PAIR, t=PAIR)
-        first_pair = dealt1[0][:].rearrange("p t m j -> p m j t")
-        nc.vector.tensor_copy(first_pair[:, SCALAR_M_PASS1:], raw_pairs[:, 0, SCALAR_M_PASS1:])
-        nc.scalar.copy(first_pair[:, :SCALAR_M_PASS1], raw_pairs[:, 0, :SCALAR_M_PASS1])
-        nc.scalar.copy(dealt1[1][:].rearrange("p t m j -> p m j t"), raw_pairs[:, 1])
+        for a, share in enumerate((40, 84)):
+            pair = dealt1[a][:].rearrange("p t m j -> p m j t")
+            nc.vector.tensor_copy(pair[:, share:], raw_pairs[:, a, share:])
+            nc.scalar.copy(pair[:, :share], raw_pairs[:, a, :share])
         quantize_w1(1, dealt1[0][:], 0)
         pick_words(1, 0, 1)
         quantize_w1(1, dealt1[1][:], PAIR)
@@ -209,14 +209,46 @@ def tile_picked_modgate_mlpsilu_p_kernel(tc, x_words, x_scales, gate, w1, w2_wor
                 window[:].indirect(entries(first, last)), y[:, first * CHUNK : last * CHUNK], scores, MULT
             )
 
+        def half_hidden(u, v, tag):
+            width = CHUNK // 2
+            h_half = keep.tile([P, width * PACK], BF16, name=f"h{u}{v}", tag=tag, align_bytes=64)
+            nc.scalar.activation(
+                h_half[:].rearrange("p (n t) -> p n t", t=PACK),
+                h_banks[u][:, :, v * width : (v + 1) * width].rearrange("p t n -> p n t"),
+                SILU,
+            )
+            return h_half
+
+        def second_product_of_halves(u, halves):
+            h_codes = keep.tile([P, CHUNK], U32, name=f"h_codes{u}", tag=f"h_codes{u}", align_bytes=64)
+            h_plane = keep.tile([P, CHUNK], U8, name=f"h_plane{u}", tag=f"h_plane{u}", align_bytes=64)
+            y_bank = psum.tile([P, CHUNK], F32, name=f"y_bank{u}", tag=f"y_bank{u}")
+            width = CHUNK // 2
+            for v, h_half in enumerate(halves):
+                cols = slice(v * width, (v + 1) * width)
+                nc.vector.quantize_mx(out=h_codes[:, cols].bitcast(FP8X4), scales=h_plane[:, cols], in_=h_half[:])
+            nc.tensor.matmul_mx(
+                out=y_bank[:],
+                lhsT=w2_codes[:].bitcast(FP8X4),
+                lhsT_scale=w2_plane[:],
+                rhs=h_codes[:].bitcast(FP8X4),
+                rhs_scale=h_plane[:],
+                start=True,
+                stop=True,
+            )
+            return y_bank
+
         h = [hidden(0, "h0", FIRST_PIECES), hidden(1, "h1")]
+        h2_first = half_hidden(2, 0, "h20")
         y_banks = [second_product(0, h[0], FIRST_PIECES), second_product(1, h[1])]
         fetch(0, y_banks[0])
         put_back(0, 1, scores_early[:, :CHUNK])
-        h.extend((hidden(2, "h_codes0"), hidden(3, "h_plane0")))
-        y_banks.extend(second_product(u, h[u]) for u in (2, 3))
+        h2_second = half_hidden(2, 1, "h_codes0")
+        h3 = hidden(3, "h_plane0")
+        y_banks.append(second_product_of_halves(2, (h2_first, h2_second)))
+        y_banks.append(second_product(3, h3))
         fetch(1, y_banks[1])
-        scores_late = pick_scores(2, CHUNKS, "h_codes0")
+        scores_late = pick_scores(2, CHUNKS, "h_codes1")
         for u in range(2, CHUNKS):
             fetch(u, y_banks[u])
         put_back(1, 2, scores_early[:, CHUNK:])

@@ -1,7 +1,6 @@
 from contextlib import ExitStack
 
 import concourse.mybir as mybir
-from concourse.masks import make_identity
 
 K, T, S, H, N = 1024, 1024, 512, 512, 128
 FLOPS = 2 * S * H * (K + N)
@@ -39,11 +38,6 @@ def tile_picked_modgate_mlpsilu_p_kernel(tc, x_words, x_scales, gate, w1, w2_wor
         x_planes = keep.tile([P, T], U8, name="x_planes", align_bytes=64)
         nc.gpsimd.memset(x_planes[:].bitcast(I32), 0)
 
-        warm_in = keep.tile([P, 1], F32, name="warm_in")
-        warm_out = keep.tile([P, 1], F32, name="warm_out")
-        nc.gpsimd.memset(warm_in[:], 0.0)
-        nc.scalar.activation(warm_out[:], warm_in[:], SILU)
-
         x_table = [keep.tile([P, T], I32, name=f"x_table{g}", align_bytes=64) for g in range(PASSES)]
         w1_raw = [keep.tile([P, PACK, H], F32, name=f"w1_raw{g}", align_bytes=64) for g in range(PASSES)]
         offsets = keep.tile([P, S // 16], U16, name="offsets")
@@ -53,18 +47,24 @@ def tile_picked_modgate_mlpsilu_p_kernel(tc, x_words, x_scales, gate, w1, w2_wor
 
         w1_rows = [w1[g * P * PACK : (g + 1) * P * PACK, :].rearrange("(p j) h -> p j h", j=PACK) for g in range(PASSES)]
 
-        load_x(0)
-        nc.sync.dma_start(offsets[:], offs)
-        gate_row = keep.tile([P, T // P], F32, name="gate_row", tag="dealt0", align_bytes=64)
-        nc.sync.dma_start(gate_row[:], gate[0].rearrange("(p c) -> p c", p=P))
         for q in range(QUADRANTS):
-            nc.sync.dma_start(
+            queue = nc.scalar if q < QUADRANTS // 2 else nc.sync
+            queue.dma_start(
                 x_planes[32 * q : 32 * q + 4 * PASSES, :].bitcast(I32),
                 x_scales[:, 4 * q : 4 * q + 4, :].bitcast(I32),
             )
+        warm_in = keep.tile([P, 1], F32, name="warm_in")
+        warm_out = keep.tile([P, 1], F32, name="warm_out")
+        nc.gpsimd.memset(warm_in[:], 0.0)
+        nc.scalar.activation(warm_out[:], warm_in[:], SILU)
+
+        load_x(0)
+        nc.sync.dma_start(offsets[:], offs)
         for g in range(PASSES):
             nc.sync.dma_start(w1_raw[g][:], w1_rows[g])
         load_x(1)
+        gate_table = keep.tile([P, T], F32, name="gate_table", align_bytes=64)
+        nc.sync.dma_start(gate_table[:], gate)
         w2_codes = keep.tile([P, N], I32, name="w2_codes", align_bytes=64)
         nc.sync.dma_start(w2_codes[:], w2_words[0].rearrange("p n t -> p (n t)").bitcast(I32))
         w2_plane = keep.tile([P, N], U8, name="w2_plane", align_bytes=64)
@@ -77,19 +77,6 @@ def tile_picked_modgate_mlpsilu_p_kernel(tc, x_words, x_scales, gate, w1, w2_wor
 
         window = keep.tile([P, T], F32, name="window", align_bytes=64)
         nc.vector.memset(window[:], 0.0)
-
-        identity = keep.tile([P, P], F32, name="identity", align_bytes=64)
-        make_identity(nc, identity[:])
-        gate_table = keep.tile([P, T], F32, name="gate_table", align_bytes=64)
-        for a in range(T // P // PACK):
-            spread = psum.tile([P, PACK, P], F32, name=f"spread{a}", tag=f"y_bank{a}")
-            for c in range(PACK):
-                column = gate_row[:, a * PACK + c : a * PACK + c + 1]
-                nc.tensor.transpose(spread[:, c, :], column.to_broadcast([P, P]), identity[:])
-            nc.scalar.copy(
-                gate_table[:].rearrange("p (n a c) -> p a n c", n=P, c=PACK)[:, a],
-                spread[:].rearrange("p c n -> p n c"),
-            )
 
         def entries(first, last):
             return offsets[:, first * LIST_COLS : last * LIST_COLS]
@@ -118,9 +105,9 @@ def tile_picked_modgate_mlpsilu_p_kernel(tc, x_words, x_scales, gate, w1, w2_wor
 
         h_banks = [psum.tile([P, PACK, CHUNK], F32, name=f"h_bank{u}") for u in range(CHUNKS)]
 
-        def first_product(u, g):
+        def first_product(u, g, tiles=range(PACK)):
             tokens = slice(u * CHUNK, (u + 1) * CHUNK)
-            for t in range(PACK):
+            for t in tiles:
                 nc.tensor.matmul_mx(
                     out=h_banks[u][:, t, :],
                     lhsT=w1_codes[g][:, t, :].bitcast(FP8X4),
@@ -131,37 +118,36 @@ def tile_picked_modgate_mlpsilu_p_kernel(tc, x_words, x_scales, gate, w1, w2_wor
                     stop=(g == PASSES - 1 and t == PACK - 1),
                 )
 
-        dealt0 = keep.tile([P, PACK, P, PACK], BF16, name="dealt0", tag="dealt0", align_bytes=64)
-        nc.scalar.copy(
-            dealt0[:].rearrange("p t m j -> p m j t")[:, :SCALAR_M_PASS0],
-            w1_raw[0][:].rearrange("p j (m t) -> p m j t", t=PACK)[:, :SCALAR_M_PASS0],
-        )
-        nc.vector.tensor_copy(
-            dealt0[:].rearrange("p (a t) m j -> p a m j t", t=PAIR)[:, :, SCALAR_M_PASS0:],
-            w1_raw[0][:].rearrange("p j (m a t) -> p a m j t", a=PACK // PAIR, t=PAIR)[:, :, SCALAR_M_PASS0:],
-        )
-        quantize_w1(0, dealt0[:], 0)
-        for u in range(CHUNKS):
-            first_product(u, 0)
+        def round_pass(g, shares):
+            dealt = [keep.tile([P, PAIR, P, PACK], BF16, name=f"dealt{g}{a}", align_bytes=64) for a in range(PACK // PAIR)]
+            raw_pairs = w1_raw[g][:].rearrange("p j (m a t) -> p a m j t", a=PACK // PAIR, t=PAIR)
+            for a, share in enumerate(shares):
+                pair = dealt[a][:].rearrange("p t m j -> p m j t")
+                nc.vector.tensor_copy(pair[:, share:], raw_pairs[:, a, share:])
+                nc.scalar.copy(pair[:, :share], raw_pairs[:, a, :share])
+            return dealt
+
+        dealt0 = round_pass(0, (44, 104))
+        for a in range(PACK // PAIR):
+            quantize_w1(0, dealt0[a][:], a * PAIR)
+        for t in range(PACK):
+            for u in range(CHUNKS):
+                first_product(u, 0, (t,))
 
         def pick_scores(first, last, tag):
             scores = keep.tile([P, (last - first) * CHUNK], F32, name=f"scores{first}", tag=tag, align_bytes=64)
             nc.scalar.activation(scores[:], gate_table[:].indirect(entries(first, last)), COPY)
             return scores
 
-        scores_early = pick_scores(0, 2, "scores_early")
 
-        dealt1 = [keep.tile([P, PAIR, P, PACK], BF16, name=f"dealt1{a}", align_bytes=64) for a in range(PACK // PAIR)]
-        raw_pairs = w1_raw[1][:].rearrange("p j (m a t) -> p a m j t", a=PACK // PAIR, t=PAIR)
-        for a, share in enumerate((40, 84)):
-            pair = dealt1[a][:].rearrange("p t m j -> p m j t")
-            nc.vector.tensor_copy(pair[:, share:], raw_pairs[:, a, share:])
-            nc.scalar.copy(pair[:, :share], raw_pairs[:, a, :share])
+        dealt1 = round_pass(1, (40, 84))
         quantize_w1(1, dealt1[0][:], 0)
         pick_words(1, 0, 1)
         quantize_w1(1, dealt1[1][:], PAIR)
         for u in range(1, CHUNKS):
             pick_words(1, u, u + 1)
+        scores0 = keep.tile([P, CHUNK], F32, name="scores0", align_bytes=64)
+        nc.vector.tensor_copy(scores0[:], gate_table[:].indirect(entries(0, 1)))
         for u in range(CHUNKS):
             first_product(u, 1)
 
@@ -240,9 +226,12 @@ def tile_picked_modgate_mlpsilu_p_kernel(tc, x_words, x_scales, gate, w1, w2_wor
 
         h = [hidden(0, "h0", FIRST_PIECES), hidden(1, "h1")]
         h2_first = half_hidden(2, 0, "h20")
-        y_banks = [second_product(0, h[0], FIRST_PIECES), second_product(1, h[1])]
+        y_banks = [second_product(0, h[0], FIRST_PIECES)]
+        scores1 = keep.tile([P, CHUNK], F32, name="scores1", tag="h0", align_bytes=64)
+        nc.vector.tensor_copy(scores1[:], gate_table[:].indirect(entries(1, 2)))
+        y_banks.append(second_product(1, h[1]))
         fetch(0, y_banks[0])
-        put_back(0, 1, scores_early[:, :CHUNK])
+        put_back(0, 1, scores0[:])
         h2_second = half_hidden(2, 1, "h_codes0")
         h3 = hidden(3, "h_plane0")
         y_banks.append(second_product_of_halves(2, (h2_first, h2_second)))
@@ -251,6 +240,6 @@ def tile_picked_modgate_mlpsilu_p_kernel(tc, x_words, x_scales, gate, w1, w2_wor
         scores_late = pick_scores(2, CHUNKS, "h_codes1")
         for u in range(2, CHUNKS):
             fetch(u, y_banks[u])
-        put_back(1, 2, scores_early[:, CHUNK:])
+        put_back(1, 2, scores1[:])
         put_back(2, CHUNKS, scores_late[:])
         nc.sync.dma_start(out, window[:])

@@ -105,6 +105,9 @@ def tile_picked_modgate_mlpsilu_p_kernel(tc, x_words, x_scales, gate, w1, w2_wor
 
         h_banks = [psum.tile([P, PACK, CHUNK], F32, name=f"h_bank{u}") for u in range(CHUNKS)]
 
+        def pass_order(u):
+            return (1, 0) if u == CHUNKS - 1 else (0, 1)
+
         def first_product(u, g, tiles=range(PACK)):
             tokens = slice(u * CHUNK, (u + 1) * CHUNK)
             for t in tiles:
@@ -114,8 +117,8 @@ def tile_picked_modgate_mlpsilu_p_kernel(tc, x_words, x_scales, gate, w1, w2_wor
                     lhsT_scale=w1_planes[g][:, t, :],
                     rhs=picked[g][:, tokens].bitcast(FP8X4),
                     rhs_scale=picked_planes[4 * g :, tokens],
-                    start=(g == 0 and t == 0),
-                    stop=(g == PASSES - 1 and t == PACK - 1),
+                    start=(g == pass_order(u)[0] and t == 0),
+                    stop=(g == pass_order(u)[-1] and t == PACK - 1),
                 )
 
         def round_pass(g, shares):
@@ -131,7 +134,7 @@ def tile_picked_modgate_mlpsilu_p_kernel(tc, x_words, x_scales, gate, w1, w2_wor
         for a in range(PACK // PAIR):
             quantize_w1(0, dealt0[a][:], a * PAIR)
         for t in range(PACK):
-            for u in range(CHUNKS):
+            for u in range(CHUNKS - 1):
                 first_product(u, 0, (t,))
 
         def pick_scores(first, last, tag):
@@ -150,6 +153,7 @@ def tile_picked_modgate_mlpsilu_p_kernel(tc, x_words, x_scales, gate, w1, w2_wor
         nc.vector.tensor_copy(scores0[:], gate_table[:].indirect(entries(0, 1)))
         for u in range(CHUNKS):
             first_product(u, 1)
+        first_product(CHUNKS - 1, 0)
 
         def hidden(u, tag, pieces=1):
             h_u = keep.tile([P, CHUNK * PACK], BF16, name=f"h{u}", tag=tag, align_bytes=64)

from contextlib import ExitStack

import concourse.mybir as mybir

K, T, S, H, N = 1024, 1024, 512, 512, 128
FLOPS = 2 * S * H * (K + N)

F32 = mybir.dt.float32
BF16 = mybir.dt.bfloat16
I32 = mybir.dt.int32
U32 = mybir.dt.uint32
U16 = mybir.dt.uint16
U8 = mybir.dt.uint8
FP8X4 = mybir.dt.float8_e4m3fn_x4
SILU = mybir.ActivationFunctionType.Silu
COPY = mybir.ActivationFunctionType.Copy
MULT = mybir.AluOpType.mult

P = 128
PACK = 4
PASSES = K // (P * PACK)
QUADRANTS = 4
CHUNK = 128
CHUNKS = S // CHUNK
LIST_COLS = CHUNK // 16
FIRST_PIECES = 2
PAIR = 2
SCALAR_M_PASS0 = 40
SCALAR_M_PASS1 = 32


def tile_picked_modgate_mlpsilu_p_kernel(tc, x_words, x_scales, gate, w1, w2_words, w2_scales, offs, out):
    nc = tc.nc
    with ExitStack() as ctx:
        keep = ctx.enter_context(tc.tile_pool(name="keep", bufs=1))
        psum = ctx.enter_context(tc.psum_pool(name="psum", bufs=1))

        x_planes = keep.tile([P, T], U8, name="x_planes", align_bytes=64)
        nc.gpsimd.memset(x_planes[:].bitcast(I32), 0)

        x_table = [keep.tile([P, T], I32, name=f"x_table{g}", align_bytes=64) for g in range(PASSES)]
        w1_raw = [keep.tile([P, PACK, H], F32, name=f"w1_raw{g}", align_bytes=64) for g in range(PASSES)]
        offsets = keep.tile([P, S // 16], U16, name="offsets")

        def load_x(g):
            nc.sync.dma_start(x_table[g][:], x_words[g].rearrange("p n t -> p (n t)").bitcast(I32))

        w1_rows = [w1[g * P * PACK : (g + 1) * P * PACK, :].rearrange("(p j) h -> p j h", j=PACK) for g in range(PASSES)]

        for q in range(QUADRANTS):
            queue = nc.scalar if q < QUADRANTS // 2 else nc.sync
            queue.dma_start(
                x_planes[32 * q : 32 * q + 4 * PASSES, :].bitcast(I32),
                x_scales[:, 4 * q : 4 * q + 4, :].bitcast(I32),
            )
        warm_in = keep.tile([P, 1], F32, name="warm_in")
        warm_out = keep.tile([P, 1], F32, name="warm_out")
        nc.gpsimd.memset(warm_in[:], 0.0)
        nc.scalar.activation(warm_out[:], warm_in[:], SILU)

        load_x(0)
        nc.sync.dma_start(offsets[:], offs)
        for g in range(PASSES):
            nc.sync.dma_start(w1_raw[g][:], w1_rows[g])
        load_x(1)
        gate_table = keep.tile([P, T], F32, name="gate_table", align_bytes=64)
        nc.sync.dma_start(gate_table[:], gate)
        w2_codes = keep.tile([P, N], I32, name="w2_codes", align_bytes=64)
        nc.sync.dma_start(w2_codes[:], w2_words[0].rearrange("p n t -> p (n t)").bitcast(I32))
        w2_plane = keep.tile([P, N], U8, name="w2_plane", align_bytes=64)
        nc.gpsimd.memset(w2_plane[:].bitcast(I32), 0)
        for q in range(QUADRANTS):
            nc.sync.dma_start(
                w2_plane[32 * q : 32 * q + 4, :].bitcast(I32),
                w2_scales[0, 4 * q : 4 * q + 4, :].bitcast(I32),
            )

        window = keep.tile([P, T], F32, name="window", align_bytes=64)
        nc.vector.memset(window[:], 0.0)

        def entries(first, last):
            return offsets[:, first * LIST_COLS : last * LIST_COLS]

        picked = [keep.tile([P, S], U32, name=f"picked{g}", align_bytes=64) for g in range(PASSES)]

        def pick_words(g, first, last):
            nc.vector.tensor_copy(
                picked[g][:, first * CHUNK : last * CHUNK], x_table[g][:].bitcast(U32).indirect(entries(first, last))
            )

        pick_words(0, 0, CHUNKS)
        picked_planes = keep.tile([P, S], U8, name="picked_planes", align_bytes=64)
        nc.vector.tensor_copy(picked_planes[:], x_planes[:].indirect(offsets[:]))

        w1_codes = [keep.tile([P, PACK, P], U32, name=f"w1_codes{g}", align_bytes=64) for g in range(PASSES)]
        w1_planes = [keep.tile([P, PACK, P], U8, name=f"w1_planes{g}", align_bytes=64) for g in range(PASSES)]

        def quantize_w1(g, dealt, first):
            for t in range(dealt.shape[1]):
                nc.vector.quantize_mx(
                    out=w1_codes[g][:, first + t, :].bitcast(FP8X4),
                    scales=w1_planes[g][:, first + t, :],
                    in_=dealt[:, t].rearrange("p m j -> p (m j)"),
                )

        h_banks = [psum.tile([P, PACK, CHUNK], F32, name=f"h_bank{u}") for u in range(CHUNKS)]

        def pass_order(u):
            return (1, 0) if u == CHUNKS - 1 else (0, 1)

        def first_product(u, g, tiles=range(PACK)):
            tokens = slice(u * CHUNK, (u + 1) * CHUNK)
            for t in tiles:
                nc.tensor.matmul_mx(
                    out=h_banks[u][:, t, :],
                    lhsT=w1_codes[g][:, t, :].bitcast(FP8X4),
                    lhsT_scale=w1_planes[g][:, t, :],
                    rhs=picked[g][:, tokens].bitcast(FP8X4),
                    rhs_scale=picked_planes[4 * g :, tokens],
                    start=(g == pass_order(u)[0] and t == 0),
                    stop=(g == pass_order(u)[-1] and t == PACK - 1),
                )

        def round_pass(g, shares):
            dealt = [keep.tile([P, PAIR, P, PACK], BF16, name=f"dealt{g}{a}", align_bytes=64) for a in range(PACK // PAIR)]
            raw_pairs = w1_raw[g][:].rearrange("p j (m a t) -> p a m j t", a=PACK // PAIR, t=PAIR)
            for a, share in enumerate(shares):
                pair = dealt[a][:].rearrange("p t m j -> p m j t")
                nc.vector.tensor_copy(pair[:, share:], raw_pairs[:, a, share:])
                nc.scalar.copy(pair[:, :share], raw_pairs[:, a, :share])
            return dealt

        dealt0 = round_pass(0, (44, 104))
        for a in range(PACK // PAIR):
            quantize_w1(0, dealt0[a][:], a * PAIR)
        for t in range(PACK):
            for u in range(CHUNKS - 1):
                first_product(u, 0, (t,))

        def pick_scores(first, last, tag):
            scores = keep.tile([P, (last - first) * CHUNK], F32, name=f"scores{first}", tag=tag, align_bytes=64)
            nc.scalar.activation(scores[:], gate_table[:].indirect(entries(first, last)), COPY)
            return scores


        dealt1 = round_pass(1, (40, 84))
        quantize_w1(1, dealt1[0][:], 0)
        pick_words(1, 0, 1)
        quantize_w1(1, dealt1[1][:], PAIR)
        for u in range(1, CHUNKS):
            pick_words(1, u, u + 1)
        scores0 = keep.tile([P, CHUNK], F32, name="scores0", align_bytes=64)
        nc.vector.tensor_copy(scores0[:], gate_table[:].indirect(entries(0, 1)))
        for u in range(CHUNKS):
            first_product(u, 1)
        first_product(CHUNKS - 1, 0)

        def hidden(u, tag, pieces=1):
            h_u = keep.tile([P, CHUNK * PACK], BF16, name=f"h{u}", tag=tag, align_bytes=64)
            width = CHUNK // pieces
            for v in range(pieces):
                nc.scalar.activation(
                    h_u[:, v * width * PACK : (v + 1) * width * PACK].rearrange("p (n t) -> p n t", t=PACK),
                    h_banks[u][:, :, v * width : (v + 1) * width].rearrange("p t n -> p n t"),
                    SILU,
                )
            return h_u

        def second_product(u, h_u, pieces=1):
            h_codes = keep.tile([P, CHUNK], U32, name=f"h_codes{u}", tag=f"h_codes{u}", align_bytes=64)
            h_plane = keep.tile([P, CHUNK], U8, name=f"h_plane{u}", tag=f"h_plane{u}", align_bytes=64)
            y_bank = psum.tile([P, CHUNK], F32, name=f"y_bank{u}", tag=f"y_bank{u}")
            width = CHUNK // pieces
            for v in range(pieces):
                cols = slice(v * width, (v + 1) * width)
                nc.vector.quantize_mx(
                    out=h_codes[:, cols].bitcast(FP8X4),
                    scales=h_plane[:, cols],
                    in_=h_u[:, v * width * PACK : (v + 1) * width * PACK],
                )
                nc.tensor.matmul_mx(
                    out=y_bank[:, cols],
                    lhsT=w2_codes[:].bitcast(FP8X4),
                    lhsT_scale=w2_plane[:],
                    rhs=h_codes[:, cols].bitcast(FP8X4),
                    rhs_scale=h_plane[:, cols],
                    start=True,
                    stop=True,
                )
            return y_bank

        y = keep.tile([P, S], F32, name="y", align_bytes=64)

        def fetch(u, y_bank):
            nc.scalar.copy(y[:, u * CHUNK : (u + 1) * CHUNK], y_bank[:])

        def put_back(first, last, scores):
            nc.vector.tensor_tensor(
                window[:].indirect(entries(first, last)), y[:, first * CHUNK : last * CHUNK], scores, MULT
            )

        def half_hidden(u, v, tag):
            width = CHUNK // 2
            h_half = keep.tile([P, width * PACK], BF16, name=f"h{u}{v}", tag=tag, align_bytes=64)
            nc.scalar.activation(
                h_half[:].rearrange("p (n t) -> p n t", t=PACK),
                h_banks[u][:, :, v * width : (v + 1) * width].rearrange("p t n -> p n t"),
                SILU,
            )
            return h_half

        def second_product_of_halves(u, halves):
            h_codes = keep.tile([P, CHUNK], U32, name=f"h_codes{u}", tag=f"h_codes{u}", align_bytes=64)
            h_plane = keep.tile([P, CHUNK], U8, name=f"h_plane{u}", tag=f"h_plane{u}", align_bytes=64)
            y_bank = psum.tile([P, CHUNK], F32, name=f"y_bank{u}", tag=f"y_bank{u}")
            width = CHUNK // 2
            for v, h_half in enumerate(halves):
                cols = slice(v * width, (v + 1) * width)
                nc.vector.quantize_mx(out=h_codes[:, cols].bitcast(FP8X4), scales=h_plane[:, cols], in_=h_half[:])
            nc.tensor.matmul_mx(
                out=y_bank[:],
                lhsT=w2_codes[:].bitcast(FP8X4),
                lhsT_scale=w2_plane[:],
                rhs=h_codes[:].bitcast(FP8X4),
                rhs_scale=h_plane[:],
                start=True,
                stop=True,
            )
            return y_bank

        h = [hidden(0, "h0", FIRST_PIECES), hidden(1, "h1")]
        h2_first = half_hidden(2, 0, "h20")
        y_banks = [second_product(0, h[0], FIRST_PIECES)]
        scores1 = keep.tile([P, CHUNK], F32, name="scores1", tag="h0", align_bytes=64)
        nc.vector.tensor_copy(scores1[:], gate_table[:].indirect(entries(1, 2)))
        y_banks.append(second_product(1, h[1]))
        fetch(0, y_banks[0])
        put_back(0, 1, scores0[:])
        h2_second = half_hidden(2, 1, "h_codes0")
        h3 = hidden(3, "h_plane0")
        y_banks.append(second_product_of_halves(2, (h2_first, h2_second)))
        y_banks.append(second_product(3, h3))
        fetch(1, y_banks[1])
        scores_late = pick_scores(2, CHUNKS, "h_codes1")
        for u in range(2, CHUNKS):
            fetch(u, y_banks[u])
        put_back(1, 2, scores1[:])
        put_back(2, CHUNKS, scores_late[:])
        nc.sync.dma_start(out, window[:])
